import numpy as np, ml_dtypes
CORES = [40,41,42,43,44,45,46,47]
N = 8
import mx_ref
BF = ml_dtypes.bfloat16
def tile(rs):
    return np.stack(rs, axis=2).reshape(128, -1).astype(BF)
def pick(q, e):
    c = np.concatenate([q[0].reshape(128, -1, 4), np.zeros((128, 1, 4), np.uint8)], axis=1); s = np.concatenate([q[1], np.ones((16, 1), np.uint8)], axis=1)
    return (np.ascontiguousarray(c[:, e].reshape(128, -1)), np.ascontiguousarray(s[:, e]))
def join(*qs):
    return (np.concatenate([q[0] for q in qs], axis=1), np.concatenate([q[1] for q in qs], axis=1))
def put(q, e, v):
    c, s = q[0].reshape(128, -1, 4).copy(), q[1].copy(); c[:, e] = v[0].reshape(128, -1, 4); s[:, e] = v[1]
    return (c.reshape(128, -1), s)
def pk(c, s):
    return (np.ascontiguousarray(c), mx_ref.live(s))
def emit(q):
    return q[0], q[1]
def packed(v, rng):
    q = [mx_ref.quantize(np.ascontiguousarray(v[r])) for r in range(N)]
    return np.stack([a for a, b in q]), np.stack([mx_ref.plane(b, rng) for a, b in q])
def values_of_codes():
    e, c = np.zeros((128, 128, 4), np.float32), np.zeros((128, 2, 4), np.uint8)
    e[np.arange(128), np.arange(128), 0] = 1
    c[:127, :, 0] = np.arange(256).reshape(2, 128).T[:127]
    return mx_ref.matmul(mx_ref.quantize(e.reshape(128, 512).astype(BF)), (c.reshape(128, 8), np.full((16, 2), 127, np.uint8))).T.reshape(-1).astype(np.float64)
CODE_VALUE, SCALE_VALUE = values_of_codes(), 2.0 ** (np.arange(256) - 127.0)
def decode(q):
    return (CODE_VALUE[q[0]].reshape(16, 8, -1, 4) * SCALE_VALUE[q[1]][:, None, :, None] + 0.0).reshape(128, -1).astype(np.float32)
def f(rng, *shape):
    return mx_ref.flush((rng.standard_normal(shape, dtype=np.float32) * np.exp2(rng.integers(-2, 3, shape[:-1] + (1,)))).astype(BF))
def wide(rng, *shape, cols=0):
    v = rng.standard_normal(shape, dtype=np.float32) * np.exp2(rng.integers(-12, 13, shape)).astype(np.float32)
    if cols: v *= np.repeat(np.exp2(rng.integers(-cols, cols + 1, shape[:-2] + (1, shape[-1] // 4))) * (rng.random(shape[:-2] + (1, shape[-1] // 4)) > 0.0625), 4, axis=-1).astype(np.float32)
    return mx_ref.flush(v.astype(BF))
C, M, P, V, K, R = 384, 16, 24, 6, 18, 3
def numbers_of(rng):
    return {"x": np.array(f(rng, N, 128, 4 * C)), "u": np.array(f(rng, N, 128, 512)), "v": np.array(f(rng, N, 128, 512))}
def weights(rng, w):
    c, p = packed(np.ascontiguousarray(w).reshape(N, 128, 2048), rng)
    return {"wc": c, "ws": p}
def layers(rng, still=[]):
    w = np.array(f(rng, N, 128, 2048)).reshape(N, 8, 16, 4, 8, 16, 4)
    for i in still:
        w[:, :, i] = 0
        w[:, :, :, :, :, i] = 0
    return weights(rng, w)
def setup_inputs(rng):
    return {**numbers_of(rng), **layers(rng)}
def setup_inputs_ties(rng):
    d = numbers_of(rng)
    x = d["x"].reshape(N, 8, 16, C, 4)
    x[:, :, 0] = 0
    x[:, :, 0, :, 0] = rng.integers(1, 4, (N, 8, C)).astype(np.float32).astype(BF)
    u = d["u"].reshape(N, 128, 128, 4)
    u[:, :, ::16] = 0
    o = rng.permutation(N)
    for r in range(N):
        for h in range(0, 128, 16): u[r, h, h, 0] = 0.0 if r == o[0] else -1.0 if r == o[1] else 1.0
    return {"x": x.reshape(N, 128, 4 * C), "u": u.reshape(N, 128, 512), "v": d["v"], **layers(rng, [0])}
def setup_inputs_near(rng):
    d = numbers_of(rng)
    x = d["x"].astype(np.float32).reshape(N, 8, 16, C, 4)
    x[:, :, 0] = 0
    x[:, :, 8:] = 0
    s = rng.integers(0, 16, (N, 8, C))
    x[:, :, 8] = ((s[:, :, :, None] >> np.arange(4)) & 1) * np.exp2(np.arange(4) - 23.0)
    u = d["u"].reshape(N, 128, 128, 4)
    u[:, :, ::16] = 0
    o = rng.permutation(N) % 4
    for r in range(N):
        if o[r] < 2:
            x[r, :, 0, :, 0] = np.repeat(rng.integers(0, 2, P) * 2.0 - 1.0, M)
            x[r, :, 11, :, 0] = 2.0 ** -10
        elif o[r] == 2:
            a = rng.permutation(M)
            x[r, :, 0, int(a[0])::M, 0] = 1.0
            x[r, :, 0, int(a[1])::M, 0] = -1.0
        else:
            x[r, :, 8] = 0
            x[r, :, 10, :, 0] = (1.0 + 0.125 * rng.integers(0, 2, (8, C))) * 2.0 ** -30
            for g in rng.permutation(8)[:4]: x[r, g, 0, rng.integers(C), 0] = 2.0 ** 30
        k = 1.0 if o[r] == 0 else 2.0 ** -30
        for h in range(0, 128, 16):
            u[r, h, h, 0] = k if o[r] < 2 else 1.0
            if o[r] < 3: u[r, h + 8, h] = k
            else: u[r, h + 10, h, 0] = k
            if o[r] < 2: u[r, h + 11, h, 0] = k
    return {"x": x.reshape(N, 128, 4 * C).astype(BF), "u": u.reshape(N, 128, 512), "v": d["v"], **layers(rng, [0, 8, 9, 10, 11, 12, 13, 14, 15])}
def setup_inputs_huge(rng):
    d = numbers_of(rng)
    c = rng.choice([-1.0, 1.0], (N, P, M))
    c[:, ::2] = -1.0
    e = rng.integers(N)
    x = 0.7 + 0.25 * rng.random((N, 8, 16, C, 4))
    x[e] = np.where(x[e] < 0.74, 0.875, 0.9375)
    a = 1.0 - 0.1 * rng.random((N, 128, 8, 4))
    a[e] = 1.0
    u = d["u"].reshape(N, 128, 128, 4)
    u[:, :, ::16] = (2.0 ** 30 * a).astype(np.float32).astype(BF)
    w = np.zeros((N, 128, 4, 128, 4), np.float32)
    i = np.arange(128)
    for b in range(4): w[:, i, b, i, b] = -1
    x = (2.0 ** 30 * x * c.reshape(N, 1, 1, C, 1)).astype(np.float32).astype(BF)
    return {"x": x.reshape(N, 128, 4 * C), "u": u.reshape(N, 128, 512), "v": d["v"], **weights(rng, w.astype(BF))}
def setup_inputs_deep(rng):
    d = numbers_of(rng)
    x = d["x"].reshape(N, 8, 16, C, 4)
    u = d["u"].reshape(N, 128, 128, 4)
    k = rng.integers(-2, 3, (N, 8, 1, C, 1))
    s = rng.choice([-1.0, 1.0], (N, 8, 8, C, 4)) * (1.0 + (2 * rng.integers(0, 64, (N, 8, 8, C, 4)) + 1) * 2.0 ** -7) * np.exp2(k - rng.integers(8, 15, (N, 8, 8, C, 4)))
    s[:, :, 0, :, 0] = 1.96875 * np.exp2(k[:, :, 0, :, 0])
    x[:, :, 8:] = s.astype(np.float32).astype(BF)
    a = 1.0 + 0.125 * rng.integers(0, 8, (8, C))
    g = np.arange(8)[:, None]
    e = rng.permutation(N)
    for i, t in enumerate((np.exp2(g) * a, np.exp2(7 - g) * a, np.exp2(np.arange(C) % M * 8 // M) * a, -np.exp2(g) * a)):
        x[e[i], :, 0] = 0
        x[e[i], :, 0, :, 0] = t.astype(np.float32).astype(BF)
        u[e[i], :, ::16] = 0
        for h in range(0, 128, 16): u[e[i], h, h, 0] = 1
    return {"x": x.reshape(N, 128, 4 * C), "u": u.reshape(N, 128, 512), "v": d["v"], **layers(rng, [0])}
def setup_inputs_spread(rng):
    d = setup_inputs(rng)
    d["x"] = wide(rng, N, 128, 4 * C, cols=6)
    return d
def check_inputs(d):
    b = []
    for k in ("x", "u", "v"):
        a = np.abs(d[k].astype(np.float32))
        if not (np.isfinite(a).all() and ((a == 0) | (a >= 2.0 ** -30) & (a <= 2.0 ** 30)).all()): b.append("a value of " + k)
    none, least, most = [emit(mx_ref.quantize(np.full((128, 16), k, np.float32).astype(BF)))[1][0, 0] for k in (0.0, 2.0 ** -30, 2.0 ** 30)]
    for r in range(N):
        if ((d["wc"][r] == 0x7F) | (d["wc"][r] == 0xFF)).any(): b.append("wc: a code that is no number")
        s = mx_ref.live(d["ws"][r])
        if ((s != none) & ((s < least) | (s > most))).any(): b.append("ws: a scale out of range")
    return b
def parts(t):
    return t.reshape(8, 16, -1, 4).transpose(0, 2, 1, 3)
def laid(a):
    return np.ascontiguousarray(a.transpose(0, 2, 1, 3)).reshape(128, -1)
def voids(key):
    at, out = np.repeat(np.arange(8 * C).reshape(1, 8, P, M), N, axis=0), []
    for n in range(V):
        m = np.argmax(key, axis=3)[:, :, :, None]
        a, b = np.take_along_axis(key, m, axis=3), np.take_along_axis(at, m, axis=3)
        out.append(b[:, 0, :, 0])
        waste = np.repeat((8 * C + P * n + np.arange(P)).reshape(1, 1, P, 1), N, axis=0)
        np.put_along_axis(key, m, np.concatenate([a[:, 1:], np.full((N, 1, P, 1), -np.inf, np.float32)], axis=1), axis=3)
        np.put_along_axis(at, m, np.concatenate([b[:, 1:], waste], axis=1), axis=3)
    return at.reshape(N, 8, C), np.concatenate(out, axis=1)
def reference(x, u, v, wc, ws):
    qu = [mx_ref.quantize(u[r]) for r in range(N)]
    lay = [[pick(pk(wc[r], ws[r]), np.arange(128 * b, 128 * b + 128)) for b in range(4)] for r in range(N)]
    now = [x[r] for r in range(N)]
    for t in range(R):
        key = np.stack([mx_ref.matmul(qu[r], mx_ref.quantize(now[r]))[::16] for r in range(N)]) + np.float32(0.0)
        at, drawn = voids(key.reshape(N, 8, P, M))
        have = [parts(now[r]).reshape(8 * C, 16, 4) for r in range(N)]
        ore = [mx_ref.quantize(laid(have[r][drawn[r]].reshape(K, 8, 16, 4).transpose(1, 0, 2, 3))) for r in range(N)]
        new = []
        for r in range(N):
            q = mx_ref.quantize(decode(ore[(r - t - 1) % N]).astype(BF))
            h = tile([mx_ref.matmul(lay[r][b], q) * np.float32(0.03125) for b in range(4)])
            z = laid(np.concatenate([have[r], parts(h).transpose(1, 0, 2, 3).reshape(8 * K, 16, 4)])[at[r]])
            q = mx_ref.quantize(z)
            new.append(tile([mx_ref.matmul(lay[r][b], q) * np.float32(0.03125) + z[:, b::4].astype(np.float32) for b in range(4)]))
        now = new
    y, og = np.zeros((N, 128, C), np.float32), np.zeros((N, 8, C), np.float32)
    oc, osc = np.zeros((N, 128, 4 * C), np.uint8), np.zeros((N, 16, C), np.uint8)
    for r in range(N):
        q = mx_ref.quantize(now[r])
        y[r] = mx_ref.matmul(mx_ref.quantize(v[r]), q)
        og[r] = at[r]
        oc[r], osc[r] = emit(q)
    return {"y": y, "og": og, "oc": oc, "osc": osc}

@@ -1,0 +1,474 @@
+import numpy as np
+from concourse.bass import DstId, RemoteDMATransfer
+from concourse.mybir import dt, AluOpType, ActivationFunctionType
+
+R, V, C = 3, 6, 384
+SL = 4 * C
+PAD = 16
+X0 = PAD + SL
+HB = PAD + 13 * SL
+NB = 22
+HW = 4 * NB
+WIN = HB + 8 * HW
+BIG = 1.0e29
+QG = [0, 2, 1, 3]
+SW = 72
+HC = C // 2
+
+SCRATCH = {"ps": ("psum", [128, 4096], "float32")}
+for _d, _l in (
+        ("bfloat16", dict(win=WIN, ut=512, vt=512, zero=520, ea=520, eb=520, bt=512, dd=512, z=SL, z32=SL, x32=SL)),
+        ("float8_e4m3fn_x4", dict(uq=128, urq=128, vq=128, wq=528, xq=C, zq=C, dq=128, eq=512)),
+        ("uint8", dict(us=128, urs=128, vs=128, wp=528, xs=C, zs=C, ds=128, es=512)),
+        ("float32", dict(ci=C, mask=C, seg=C, km=C, ks=512, yt=C, pf=16, d0=64, ebuf=40, oh=32 * V, nd=64 * V, kb=128 * (V + 1),
+                         ib=SW * (V + 1), sc=SW * (V + 1), tt=16, oi=64, ot=64, lr=32, lt=32, ti=32, g1=32, g2=32)),
+        ("int32", dict(pi=8, uli=8)),
+        ("uint16", dict(ul=8, dl=2, bl=2, ob=32, oz=96))):
+    for _n, _w in _l.items():
+        SCRATCH[_n] = ("sbuf", [128, _w], _d)
+for _t in range(R):
+    SCRATCH["bq%d" % _t] = ("sbuf", [128, 128], "float8_e4m3fn_x4")
+    SCRATCH["bs%d" % _t] = ("sbuf", [128, 128], "uint8")
+    SCRATCH["lq%d" % _t] = ("sbuf", [128, 128 + NB], "float8_e4m3fn_x4")
+    SCRATCH["ls%d" % _t] = ("sbuf", [128, 128 + HW], "uint8")
+SEMAPHORES = ["cv", "ca", "ct", "cg", "sent", "lx0", "lx1", "lu", "lv", "lw", "so", "sg"] + \
+    [p + str(t) for p in ("arr", "we", "wl") for t in range(R)]
+
+A = AluOpType
+AF = ActivationFunctionType
+
+
+def rank_program(g, core, T, topo):
+    rank = T.rank_of(core)
+    if rank is None:
+        return
+    N = len(T.cores)
+    eng = {"v": g.vector, "a": g.scalar, "t": g.tensor, "g": g, "s": g.sync}
+    csem = {"v": "cv", "a": "ca", "t": "ct", "g": "cg"}
+    count = {}
+    known = {e: {} for e in eng}
+    waited = {}
+    toks = [None]
+    lastw, lastr = {}, {}
+
+    def v(name, c0=None, c1=None, st=1, p0=0, p1=128):
+        w = SCRATCH[name][1][1]
+        c0 = 0 if c0 is None else c0
+        c1 = w if c1 is None else c1
+        ap = T[name][p0:p1, c0:c1:st] if st != 1 else T[name][p0:p1, c0:c1]
+        if name == "ps":
+            return (ap, name, slice(0, 8), slice(c0 // 512 * 512, c0 // 512 * 512 + 512))
+        return (ap, name, slice(p0 // 16, (p1 + 15) // 16), slice(c0, c1, st))
+
+    def arrs(name):
+        if name not in lastw:
+            lastw[name] = np.zeros((8, SCRATCH[name][1][1]), np.int32)
+            lastr[name] = {}
+        return lastw[name], lastr[name]
+
+    def wait(e, sem, n, clock=None):
+        if known[e].get(sem, 0) < n:
+            eng[e].wait_ge(T.sem[sem], n)
+            known[e][sem] = n
+            waited[sem] = max(waited.get(sem, 0), n)
+        for s, k in (clock or {}).items():
+            if known[e].get(s, 0) < k:
+                known[e][s] = k
+
+    def deps(e, reads, writes):
+        need = set()
+        for _, name, ps, cs in reads:
+            need.update(np.unique(arrs(name)[0][ps, cs]).tolist())
+        for _, name, ps, cs in writes:
+            w, r = arrs(name)
+            need.update(np.unique(w[ps, cs]).tolist())
+            for a in r.values():
+                need.update(np.unique(a[ps, cs]).tolist())
+        need.discard(0)
+        for i in sorted(need, reverse=True):
+            sem, n, clock = toks[i]
+            wait(e, sem, count[sem] if n is None else n, clock)
+
+    def note(key, tok, reads, writes):
+        toks.append(tok)
+        i = len(toks) - 1
+        for _, name, ps, cs in reads:
+            w, r = arrs(name)
+            if key not in r:
+                r[key] = np.zeros(w.shape, np.int32)
+            r[key][ps, cs] = i
+        for _, name, ps, cs in writes:
+            w, r = arrs(name)
+            w[ps, cs] = i
+            for a in r.values():
+                a[ps, cs] = 0
+
+    def op(e, call, reads, writes):
+        writes = writes + [x for x in reads if x[1] == "ps"]
+        deps(e, reads, writes)
+        sem = csem[e]
+        if e == "g":
+            wait(e, sem, count.get(sem, 0))
+        call().then_inc(T.sem[sem], 1)
+        count[sem] = count.get(sem, 0) + 1
+        note(e, [sem, count[sem], dict(known[e])], reads, writes)
+
+    def dma(e, sem, out, in_, reads, writes):
+        deps(e, reads, writes)
+        eng[e].dma_start(out, in_).then_inc(T.sem[sem], 16)
+        count[sem] = count.get(sem, 0) + 16
+        note(sem, [sem, None, dict(known[e])], reads, writes)
+
+    def aps(*xs):
+        return [x for x in xs if isinstance(x, tuple)]
+
+    def val(x):
+        return x[0] if isinstance(x, tuple) else x
+
+    def src(x, off):
+        return x[0] if off is None else x[0].indirect(off[0])
+
+    def memset(o, c):
+        op("v", lambda: g.vector.memset(o[0], c), [], [o])
+
+    def iota(o, pat, base, cm, flt=True):
+        if flt:
+            op("g", lambda: g.iota(o[0], pat, base, cm, allow_small_or_imprecise_dtypes=True), [], [o])
+        else:
+            op("g", lambda: g.iota(o[0], pat, base, cm), [], [o])
+
+    def ts(o, i, s1, op0, s2=None, op1=None, off=None):
+        if op1 is None:
+            op("v", lambda: g.vector.tensor_scalar(o[0], src(i, off), val(s1), None, op0), aps(i, s1, off), [o])
+        else:
+            op("v", lambda: g.vector.tensor_scalar(o[0], src(i, off), val(s1), val(s2), op0, op1), aps(i, s1, s2, off), [o])
+
+    def tt(o, a, b, alu, off=None):
+        op("v", lambda: g.vector.tensor_tensor(o[0], src(a, off), b[0], alu), aps(a, b, off), [o])
+
+    def scan(o, d0, d1, init, op0, op1):
+        op("v", lambda: g.vector.tensor_tensor_scan(o[0], d0[0], d1[0], init, op0, op1), [d0, d1], [o])
+
+    def tr(o, i):
+        op("v", lambda: g.vector.transpose(o[0], i[0]), [i], [o])
+
+    def act(o, i, func, bias=0.0, scale=1.0, off=None):
+        op("a", lambda: g.scalar.activation(o[0], src(i, off), func, bias=val(bias), scale=val(scale)), aps(i, bias, scale, off), [o])
+
+    def cp(e, o, i, scale=None, off=None):
+        if e == "a":
+            act(o, i, AF.Copy, scale=1.0 if scale is None else scale, off=off)
+        elif scale is None:
+            op("v", lambda: g.vector.tensor_copy(o[0], src(i, off)), aps(i, off), [o])
+        else:
+            ts(o, i, scale, A.mult, off=off)
+
+    def quant(q, s, i):
+        op("v", lambda: g.vector.quantize_mx(q[0], s[0], i[0]), [i], [q, s])
+
+    def mm(bank, n, lq, ls, rq, rs):
+        o = v("ps", 512 * bank, 512 * bank + n)
+        op("t", lambda: g.tensor.matmul_mx(o[0], lq[0], ls[0], rq[0], rs[0], True, True), [lq, ls, rq, rs], [o])
+
+    def windows(t):
+        def one(e, sem, slot, p0, p1, q0):
+            o = v("win", PAD + slot * SL, PAD + (slot + 1) * SL, 1, p0, p1)
+            if t == 0:
+                dma(e, sem, o[0], T.x[q0:q0 + p1 - p0, :], [], [o])
+            else:
+                i = v("win", X0, X0 + SL, 1, q0, q0 + p1 - p0)
+                dma(e, sem, o[0], i[0], [i], [o])
+        one("s", "we%d" % t, 0, 16, 32, 0)
+        for d in range(1, 6):
+            one("a" if t > 0 and d in (2, 4) else "s", "we%d" % t, d + 1, 0, 32, 16 * d)
+        for d in range(1, 6):
+            one("s", "wl%d" % t, d + 7, 32, 128 - 16 * d, 32 + 16 * d)
+        one("s", "wl%d" % t, 7, 0, 32, 96)
+
+    def half(name, k, w=1, base=0):
+        return v(name, base + w * HC * k, base + w * HC * (k + 1))
+
+    for t in range(R):
+        count["arr%d" % t] = len(topo.engines(T.cores[(rank - t - 1) % N], core))
+        note("arr", ["arr%d" % t, None, {}], [], [v("lq%d" % t, 128), v("ls%d" % t, 128)])
+
+    dma("a", "lu", v("ut")[0], T.u[:, :], [], [v("ut")])
+    for k in range(2):
+        o = half("win", k, 4, X0)
+        dma("s", "lx%d" % k, o[0], T.x[:, 4 * HC * k:4 * HC * (k + 1)], [], [o])
+    windows(0)
+    dma("s", "lw", v("wq", 16)[0].bitcast(dt.uint8), T.wc[:, :], [], [v("wq", 16)])
+    dma("s", "lw", v("wp", 16)[0], T.ws[:, :], [], [v("wp", 16)])
+    dma("s", "lw", v("wq", 0, 16)[0].bitcast(dt.uint8), T.wc[:, 1984:2048], [], [v("wq", 0, 16)])
+    dma("s", "lw", v("wp", 0, 16)[0], T.ws[:, 496:512], [], [v("wp", 0, 16)])
+    dma("s", "lv", v("vt")[0], T.v[:, :], [], [v("vt")])
+
+    iota(v("pi", 0, 1), [[0, 1]], 0, 1, False)
+    iota(v("uli"), [[32, 2], [64, 2], [16, 2]], 0, 0, False)
+    iota(v("ci"), [[0, 24], [1, 16]], 0, 0)
+    memset(v("lr"), 0.0)
+    memset(v("zero"), 0.0)
+    for a in range(4):
+        iota(v("ib", 1, 64, 2, 32 * a, 32 * a + 32), [[SL, 2], [4, 16]], 2 * SL * QG[a], 64)
+    iota(v("tt", 8, 14), [[4, 6]], 0, 0)
+    iota(v("tt", 0, 8), [[-SL, 2], [1, 4]], X0, 0)
+    for h in range(2):
+        iota(v("lr", 16 * h, 16 * h + 12), [[2, 2], [8, 3], [32, 2]], h, 0)
+    for name, b in (("ea", 2), ("eb", 3)):
+        op("g", lambda: g.affine_select(v(name, 0, 514)[0], v("zero", 0, 514)[0], [[-1, 514]], A.not_equal, 1.0, b, 4),
+           [v("zero", 0, 514)], [v(name, 0, 514)])
+    p = v("pi", 0, 1)
+    ts(v("pi", 1, 2), p, 15, A.bitwise_and)
+    ts(v("pi", 2, 3), p, 4, A.arith_shift_right)
+    ts(v("pi", 3, 4), p, 7, A.bitwise_and)
+    ts(v("pi", 4, 5), p, 3, A.arith_shift_right, 3, A.bitwise_and)
+    ts(v("pi", 5, 6), p, 31, A.bitwise_and)
+    cp("v", v("ul"), v("uli"))
+    memset(v("d0"), BIG)
+    memset(v("ebuf", 0, 1), 2.0)
+    cp("v", v("pf", 0, 6), v("pi", 0, 6))
+    memset(v("d0", 0, 64, 16), -BIG)
+    memset(v("ks", C), 0.0)
+    memset(v("nd", 0, None, 2), 0.0)
+    ts(v("pf", 6, 7), v("pf", 3, 4), float(HW), A.mult, float(HB + SL - X0), A.add)
+    for k, c in enumerate((31, 64)):
+        memset(v("dl", k, k + 1), c)
+    ts(v("pf", 7, 8), v("pf", 4, 5), 32.0, A.mult, v("pf", 6, 7), A.add)
+    memset(v("sc", 64, None, SW, 96, 128), -BIG)
+    memset(v("oi", p1=32), 0.0)
+    memset(v("ot"), 0.0)
+    memset(v("win", 0, PAD), 0.0)
+    memset(v("bt", C), 0.0)
+    ts(v("mask"), v("ci"), v("pf", 1, 2), A.is_equal)
+    act(v("seg"), v("ci"), AF.Sign)
+    quant(v("uq"), v("us"), v("ut"))
+    op("v", lambda: g.vector.tensor_copy(v("urq")[0].bitcast(dt.uint32), v("uq")[0].bitcast(dt.uint32).indirect(v("ul")[0])),
+       [v("uq"), v("ul")], [v("urq")])
+    op("a", lambda: g.scalar.activation(v("urs")[0], v("us")[0].indirect(v("ul")[0]), AF.Copy), [v("us"), v("ul")], [v("urs")])
+
+    def S(n, c0, c1, st=1, p0=0, p1=128):
+        return v("sc", SW * n + c0, SW * n + c1, st, p0, p1)
+
+    def down(n, e):
+        k = 1 if n in (0, V) else 2
+        c0, o0 = (47, 65) if n == V else (15, 64)
+        cp(e, S(n, o0, o0 + k, 1, 0, 64), S(n, c0, c0 + 32 * (k - 1) + 1, 32 if k > 1 else 1, 64, 128))
+        cp(e, S(n, o0, o0 + k, 1, 64, 96), S(n, c0, c0 + 32 * (k - 1) + 1, 32 if k > 1 else 1, 32, 64))
+
+    def OH(n, h0=0, h1=2):
+        return v("oh", 32 * n + 16 * h0, 32 * n + 16 * h1)
+
+    def tops(n, h0, h1):
+        scan(S(n, 16 * h0, 16 * h1), v("d0", 16 * h0, 16 * h1), v("kb", 128 * n + 1 + 32 * h0, 128 * n + 32 * h1, 2), -BIG, A.min, A.max)
+
+    def below(n, h):
+        if h == 0:
+            ts(v("ebuf", 1, 17), S(n, 0, 16), S(n, 15, 16), A.is_lt, 1.0, A.add)
+        else:
+            ts(v("ebuf", 17, 33), S(n, 16, 32), S(n, 31, 32), A.is_lt)
+
+    def hot(n, h0, h1):
+        tt(OH(n, h0, h1), v("ebuf", 16 * h0, 16 * h1), v("ebuf", 16 * h0 + 1, 16 * h1 + 1), A.is_gt)
+
+    def keep(n):
+        tt(v("nd", 64 * n + 1, 64 * n + 64, 2), v("ebuf", 0, 32), v("ebuf", 1, 33), A.is_le)
+
+    def origin_d(e, n, h):
+        o, c = SW * (n - 1) + 2 + 32 * h, (63, 65)[h]
+        if e == "a":
+            act(v("ib", o, o + 31, 2), OH(n - 1, h, h + 1), AF.Identity, scale=S(n, c, c + 1))
+        else:
+            ts(v("ib", o, o + 31, 2), OH(n - 1, h, h + 1), S(n, c, c + 1), A.mult)
+
+    def origin_s(n, h0, h1):
+        scan(v("ib", SW * n + 32 * h0, SW * n + 32 * h1), v("nd", 64 * (n - 1) + 32 * h0, 64 * (n - 1) + 32 * h1),
+             v("ib", SW * (n - 1) + 1 + 32 * h0, SW * (n - 1) + 1 + 32 * h1), 0.0, A.mult, A.add)
+
+    def origin_p(n, h0, h1):
+        tt(v("kb", 128 * (n + 1) + 65 + 32 * h0, 128 * (n + 1) + 64 + 32 * h1, 2), OH(n, h0, h1),
+           v("ib", SW * n + 1 + 32 * h0, SW * n + 32 * h1, 2), A.mult)
+
+    def drawn(e, m):
+        for h in range(2):
+            c = 32 * (m // 4) + 16 * h + 4 * (m % 4)
+            o, i, b = v("oi", c, c + 4, 1, 0, 32), v("tt", 4 * h, 4 * h + 4, 1, 0, 32), S(m + 1, 47, 48, 1, 0, 32)
+            if e == "a":
+                act(o, i, AF.Identity, bias=b)
+            else:
+                ts(o, i, b, A.add)
+
+    def quant_x(k, lq, ls):
+        quant(half("xq", k), half("xs", k), half("win", k, 4, X0))
+        mm(k, HC, lq, ls, half("xq", k), half("xs", k))
+
+    W, WB = v("win"), v("win", 0, PAD + 7 * SL)
+    for k in range(2):
+        quant_x(k, v("urq"), v("urs"))
+    ts(v("sc", SW + 65, None, SW, 96, 128), v("tt", 8, 14, 1, 96, 128), v("pf", 7, 8, 1, 96, 128), A.add)
+    tr(v("lt"), v("lr"))
+    for t in range(R):
+        for k in range(2):
+            tt(half("km", k), v("ps", 512 * k, 512 * k + HC), half("mask", k), A.mult)
+        if t == 0:
+            ts(v("bl"), v("tt", 8, 10), v("lt", 0, 1), A.add)
+        for k in range(2):
+            scan(half("ks", k), half("seg", k), half("km", k), 0.0, A.mult, A.add)
+        tr(v("kb", 1, 64, 2), v("ks", 15, 512, 16))
+        for n in range(V - 1):
+            tops(n, 0, 2 if n == 0 else 4)
+            down(n, "a")
+            below(n, 0)
+            below(n, 1)
+            if n >= 1:
+                origin_d("a", n, 0)
+                origin_d("a", n, 1)
+                drawn("a", n - 1)
+            hot(n, 0, 2)
+            keep(n)
+            tt(v("kb", 128 * n + 2, 128 * n + 65, 2), S(n, 0, 65), OH(n), A.mult, off=v("dl", 0, 2))
+            if n >= 1:
+                origin_s(n, 0, 2)
+            scan(v("kb", 128 * (n + 1), 128 * (n + 1) + 64), v("nd", 64 * n, 64 * n + 64),
+                 v("kb", 128 * n + 1, 128 * n + 65), 0.0, A.mult, A.add)
+            origin_p(n, 0, 2)
+        n = V - 1
+        tops(n, 0, 4)
+        drawn("a", n - 1)
+        origin_d("v", n, 0)
+        below(n, 0)
+        origin_s(n, 0, 1)
+        hot(n, 0, 1)
+        origin_p(n, 0, 1)
+        tops(V, 2, 3)
+        drawn("v", n)
+        tr(v("ot", p1=32), v("oi", p1=32))
+        cp("v", v("ob"), v("ot"), off=v("bl"))
+        cp("a", v("bt", 192, 384), WB, off=v("ob", 16, 28))
+        cp("v", v("bt", 0, 192), WB, off=v("ob", 0, 12))
+        cp("v", v("bt", 0, 96, 1, 32, 64), v("bt", 96, 192, 1, 0, 32))
+        cp("a", v("bt", 0, 96, 1, 64, 96), v("bt", 192, 288, 1, 0, 32))
+        cp("v", v("bt", 0, 96, 1, 96, 128), v("bt", 288, 384, 1, 0, 32))
+        bq, bs, lq, ls = "bq%d" % t, "bs%d" % t, "lq%d" % t, "ls%d" % t
+        quant(v(bq), v(bs), v("bt"))
+        to = T.cores[(rank + t + 1) % N]
+        rid, pid, _ = topo.addr(to)
+        es = topo.engines(core, to)
+        hf = len(es) // 2
+        masks = [sum(1 << k for k in es[:hf]), sum(1 << k for k in es[hf:])]
+        deps("g", [v(bq), v(bs)], [])
+        g.remote_dma_fused([
+            RemoteDMATransfer(dst_ids=[DstId(rid=rid, pnc=pid)], dma_engine_mask=masks[0], remote_sem=T.sem["arr%d" % t],
+                              src=v(bq, 0, NB)[0].bitcast(dt.uint8), dst=v(lq, 128)[0].bitcast(dt.uint8)),
+            RemoteDMATransfer(dst_ids=[DstId(rid=rid, pnc=pid)], dma_engine_mask=masks[1], remote_sem=T.sem["arr%d" % t],
+                              src=v(bs, 0, HW)[0], dst=v(ls, 128)[0])], local_sem=T.sem["sent"])
+        count["sent"] = count.get("sent", 0) + len(es)
+        if t == 0:
+            quant(v(lq, 0, 128), v(ls, 0, 128), v("zero", 0, 512))
+            for b in range(4):
+                o = 2 - 2 * (b // 2)
+                quant(v("eq", 128 * b, 128 * b + 128), v("es", 128 * b, 128 * b + 128), v("eb" if b % 2 else "ea", o, o + 512))
+            memset(v("dd"), 0.0)
+            ts(v("pf", 8, 9), v("pf", 2, 3), float(-SL), A.mult, float(X0), A.add)
+            ts(v("pf", 11, 12), v("pf", 2, 3), 2.0, A.is_ge, float(6 * SL), A.mult)
+        down(n, "v")
+        below(n, 1)
+        origin_d("v", n, 1)
+        hot(n, 1, 2)
+        origin_s(n, 1, 2)
+        keep(n)
+        origin_p(n, 1, 2)
+        down(V, "v")
+        tops(V, 3, 4)
+        origin_d("v", V, 1)
+        origin_d("v", V, 0)
+        origin_s(V, 0, 2)
+        for a in range(4):
+            tr(v("ti", 0, 32, 1, 32 * QG[a], 32 * QG[a] + 32), v("ib", SW * V + 1, SW * V + 64, 2, 32 * a, 32 * a + 32))
+        ts(v("g1", 0, 24), v("ti", 0, 24), v("pf", 8, 9), A.add)
+        ts(v("g2", 0, 24), v("g1", 0, 24), float(X0 + SL), A.is_ge, v("pf", 11, 12), A.mult)
+        tt(v("ti", 0, 24), v("g1", 0, 24), v("g2", 0, 24), A.add)
+        for k in range(4):
+            ts(v("oz", 24 * k, 24 * k + 24), v("ti", 0, 24), float(k), A.add)
+        if t == 0:
+            for k in range(1, R):
+                quant(v("lq%d" % k, 0, 128), v("ls%d" % k, 0, 128), v("zero", 0, 512))
+        if t == 1:
+            quant(v("vq"), v("vs"), v("vt"))
+            ts(v("pf", 9, 10), v("pf", 7, 8), -6.0, A.mult, float(8 * C), A.add)
+            ts(v("pf", 10, 11), v("pf", 9, 10), v("pf", 5, 6), A.add)
+        if t == R - 1:
+            fin = v("ib", SW * V + 1, SW * V + 64, 2)
+            act(v("g1"), fin, AF.Abs, bias=v("pf", 10, 11), scale=6.0)
+            ts(v("g2"), fin, 0.25, A.mult)
+            tt(v("g2"), v("g2"), v("g1"), A.min)
+            for a in range(4):
+                for h in range(2):
+                    i = v("g2", 16 * h, 16 * h + 16, 1, 32 * a, 32 * a + 24)
+                    gg = 2 * QG[a] + h
+                    dma("s", "sg", T.og[gg:gg + 1, :], i[0], [i], [])
+        for b in range(4):
+            mm(4 + b, 128, v("eq", 128 * b, 128 * b + 128), v("es", 128 * b, 128 * b + 128), v(lq, NB, NB + 128), v(ls, NB, NB + 128))
+        for b in range(4):
+            cp("va"[b % 2], v("dd", b, HW, 4), v("ps", 512 * (4 + b) + 128 - NB, 512 * (4 + b) + 128))
+        quant(v("dq"), v("ds"), v("dd"))
+        for k in range(8):
+            c = 128 * (k % 4) + 16 * (k // 4)
+            mm(k, 128, v("wq", c, c + 128), v("wp", c, c + 128), v("dq"), v("ds"))
+        h3 = HB + 6 * HW
+        for k in range(8):
+            c = h3 + HW * (k // 4)
+            cp("av"[k % 2], v("win", c + k % 4, c + HW, 4), v("ps", 512 * k, 512 * k + NB), scale=0.03125)
+        for a in range(3):
+            cp("vav"[a], v("win", HB + 2 * HW * a, HB + 2 * HW * (a + 1), 1, 96, 128), v("win", h3, h3 + 2 * HW, 1, 32 * a, 32 * a + 32))
+
+        def fill(e, k, b):
+            cp(e, v("z", 4 * HC * k + b, 4 * HC * (k + 1), 4), W, off=v("oz", 24 * b + 12 * k, 24 * b + 12 * k + 12))
+
+        def layer(k):
+            quant(half("zq", k), half("zs", k), half("z", k, 4))
+            for b in range(4):
+                mm(4 * k + b, HC, v("wq", 16 + 128 * b, 144 + 128 * b), v("wp", 16 + 128 * b, 144 + 128 * b), half("zq", k), half("zs", k))
+
+        def add(k, b):
+            c0, c1, bank = 4 * HC * k + b, 4 * HC * (k + 1), 512 * (4 * k + b)
+            tt(v("x32", c0, c1, 4), v("ps", bank, bank + HC), v("z32", c0, c1, 4), A.add)
+
+        def scale(e, c0, c1):
+            cp(e, v("win", X0 + c0, X0 + c1), v("x32", c0, c1), scale=0.03125)
+
+        for e, k, b in (("a", 0, 1), ("v", 0, 0), ("a", 0, 3), ("v", 0, 2), ("a", 1, 1)):
+            fill(e, k, b)
+        layer(0)
+        for e, k, b in (("v", 1, 0), ("a", 1, 3), ("a", 1, 2)):
+            fill(e, k, b)
+        cp("v", half("z32", 0, 4), half("z", 0, 4), scale=32.0)
+        cp("a", half("z32", 1, 4), half("z", 1, 4), scale=32.0)
+        add(0, 0)
+        add(0, 1)
+        layer(1)
+        add(0, 2)
+        add(0, 3)
+        scale("a", 0, 4 * HC)
+        for b in range(4):
+            add(1, b)
+        scale("a", 4 * HC, 6 * HC)
+        scale("v", 6 * HC, 8 * HC)
+        if t < R - 1:
+            windows(t + 1)
+        for k in range(2):
+            if t < R - 1:
+                quant_x(k, v("urq"), v("urs"))
+            else:
+                quant_x(k, v("vq"), v("vs"))
+
+    dma("s", "so", T.oc[:, :], v("xq")[0].bitcast(dt.uint8), [v("xq")], [])
+    for k in range(4):
+        i = v("xs", 0, C, 1, 32 * k, 32 * k + 4)
+        dma("aass"[k], "so", T.osc[4 * k:4 * k + 4, :], i[0], [i], [])
+    for k in range(2):
+        cp("v", half("yt", k), v("ps", 512 * k, 512 * k + HC))
+    dma("a", "so", T.y[:, :], v("yt")[0], [v("yt")], [])
+    for sem in SEMAPHORES:
+        if count.get(sem, 0) > waited.get(sem, 0):
+            e = "g" if sem == "sent" else "s"
+            eng[e].wait_ge(T.sem[sem], count[sem])

@@ -10,20 +10,21 @@ HB = PAD + 13 * SL
 NB = 22
 HW = 4 * NB
 WIN = HB + 8 * HW
-BIG = 1.0e29
+BIG = 2.0 ** 96
 QG = [0, 2, 1, 3]
-SW = 72
-HC = C // 2
+SW = 136
+CUT = [0, 256, C]
 
 SCRATCH = {"ps": ("psum", [128, 4096], "float32")}
 for _d, _l in (
         ("bfloat16", dict(win=WIN, ut=512, vt=512, zero=520, ea=520, eb=520, bt=512, dd=512, z=SL, z32=SL, x32=SL)),
         ("float8_e4m3fn_x4", dict(uq=128, urq=128, vq=128, wq=528, xq=C, zq=C, dq=128, eq=512)),
         ("uint8", dict(us=128, urs=128, vs=128, wp=528, xs=C, zs=C, ds=128, es=512)),
-        ("float32", dict(ci=C, mask=C, seg=C, km=C, ks=512, yt=C, pf=16, d0=64, ebuf=40, oh=32 * V, nd=64 * V, kb=128 * (V + 1),
-                         ib=SW * (V + 1), sc=SW * (V + 1), tt=16, oi=64, ot=64, lr=32, lt=32, ti=32, g1=32, g2=32)),
+        ("float32", dict(ci=C, mask=C, seg=C, km=C, ks=512, yt=C, pf=16, d0=128, d1=32, ebuf=40, oh=32 * V, ohn=32 * V, kc=32 * V,
+                         ic=32 * (V + 1), kb=128 * (V + 1), ib=64 * (V + 1), sc=SW * (V + 1), tt=16, oi=64, ot=64,
+                         lr=32, lt=32, ti=32, g1=32, g2=32)),
         ("int32", dict(pi=8, uli=8)),
-        ("uint16", dict(ul=8, dl=2, bl=2, ob=32, oz=96))):
+        ("uint16", dict(ul=8, bl=2, ob=32, oz=96))):
     for _n, _w in _l.items():
         SCRATCH[_n] = ("sbuf", [128, _w], _d)
 for _t in range(R):
@@ -186,7 +187,10 @@ def rank_program(g, core, T, topo):
         one("s", "wl%d" % t, 7, 0, 32, 96)
 
     def half(name, k, w=1, base=0):
-        return v(name, base + w * HC * k, base + w * HC * (k + 1))
+        return v(name, base + w * CUT[k], base + w * CUT[k + 1])
+
+    def bank(b, k):
+        return v("ps", 512 * b, 512 * b + CUT[k + 1] - CUT[k])
 
     for t in range(R):
         count["arr%d" % t] = len(topo.engines(T.cores[(rank - t - 1) % N], core))
@@ -195,7 +199,7 @@ def rank_program(g, core, T, topo):
     dma("a", "lu", v("ut")[0], T.u[:, :], [], [v("ut")])
     for k in range(2):
         o = half("win", k, 4, X0)
-        dma("s", "lx%d" % k, o[0], T.x[:, 4 * HC * k:4 * HC * (k + 1)], [], [o])
+        dma("s", "lx%d" % k, o[0], T.x[:, 4 * CUT[k]:4 * CUT[k + 1]], [], [o])
     windows(0)
     dma("s", "lw", v("wq", 16)[0].bitcast(dt.uint8), T.wc[:, :], [], [v("wq", 16)])
     dma("s", "lw", v("wp", 16)[0], T.ws[:, :], [], [v("wp", 16)])
@@ -209,7 +213,7 @@ def rank_program(g, core, T, topo):
     memset(v("lr"), 0.0)
     memset(v("zero"), 0.0)
     for a in range(4):
-        iota(v("ib", 1, 64, 2, 32 * a, 32 * a + 32), [[SL, 2], [4, 16]], 2 * SL * QG[a], 64)
+        iota(v("ib", 0, 64, 2, 32 * a, 32 * a + 32), [[SL, 2], [4, 16]], 2 * SL * QG[a], 64)
     iota(v("tt", 8, 14), [[4, 6]], 0, 0)
     iota(v("tt", 0, 8), [[-SL, 2], [1, 4]], X0, 0)
     for h in range(2):
@@ -225,19 +229,19 @@ def rank_program(g, core, T, topo):
     ts(v("pi", 5, 6), p, 31, A.bitwise_and)
     cp("v", v("ul"), v("uli"))
     memset(v("d0"), BIG)
-    memset(v("ebuf", 0, 1), 2.0)
+    memset(v("ebuf", 0, 1), BIG)
+    memset(v("d1"), BIG)
     cp("v", v("pf", 0, 6), v("pi", 0, 6))
-    memset(v("d0", 0, 64, 16), -BIG)
     memset(v("ks", C), 0.0)
-    memset(v("nd", 0, None, 2), 0.0)
+    memset(v("ib", 1, 64, 2), 0.0)
+    memset(v("d0", 0, 128, 32), -4 * BIG)
+    memset(v("d1", 0, 32, 16), -4 * BIG)
     ts(v("pf", 6, 7), v("pf", 3, 4), float(HW), A.mult, float(HB + SL - X0), A.add)
-    for k, c in enumerate((31, 64)):
-        memset(v("dl", k, k + 1), c)
-    ts(v("pf", 7, 8), v("pf", 4, 5), 32.0, A.mult, v("pf", 6, 7), A.add)
-    memset(v("sc", 64, None, SW, 96, 128), -BIG)
+    memset(v("sc", 128, None, SW, 96, 128), -BIG)
     memset(v("oi", p1=32), 0.0)
     memset(v("ot"), 0.0)
     memset(v("win", 0, PAD), 0.0)
+    ts(v("pf", 7, 8), v("pf", 4, 5), 32.0, A.mult, v("pf", 6, 7), A.add)
     memset(v("bt", C), 0.0)
     ts(v("mask"), v("ci"), v("pf", 1, 2), A.is_equal)
     act(v("seg"), v("ci"), AF.Sign)
@@ -249,49 +253,63 @@ def rank_program(g, core, T, topo):
     def S(n, c0, c1, st=1, p0=0, p1=128):
         return v("sc", SW * n + c0, SW * n + c1, st, p0, p1)
 
-    def down(n, e):
-        k = 1 if n in (0, V) else 2
-        c0, o0 = (47, 65) if n == V else (15, 64)
-        cp(e, S(n, o0, o0 + k, 1, 0, 64), S(n, c0, c0 + 32 * (k - 1) + 1, 32 if k > 1 else 1, 64, 128))
-        cp(e, S(n, o0, o0 + k, 1, 64, 96), S(n, c0, c0 + 32 * (k - 1) + 1, 32 if k > 1 else 1, 32, 64))
+    def top(n, h):
+        return (16 if n == 0 else 32) * (h + 1) - 1
 
-    def OH(n, h0=0, h1=2):
-        return v("oh", 32 * n + 16 * h0, 32 * n + 16 * h1)
+    def down(n, e, k):
+        c = 95 if k else top(n, 0)
+        cp(e, S(n, 128 + k, 129 + k, 1, 0, 64), S(n, c, c + 1, 1, 64, 128))
+        cp(e, S(n, 128 + k, 129 + k, 1, 64, 96), S(n, c, c + 1, 1, 32, 64))
 
-    def tops(n, h0, h1):
-        scan(S(n, 16 * h0, 16 * h1), v("d0", 16 * h0, 16 * h1), v("kb", 128 * n + 1 + 32 * h0, 128 * n + 32 * h1, 2), -BIG, A.min, A.max)
+    def row(name, n, h0=0, h1=2):
+        return v(name, 32 * n + 16 * h0, 32 * n + 16 * h1)
+
+    def pair(name, c, k, h0=0, h1=2):
+        return v(name, c + 32 * h0 + k, c + 32 * h1, 2)
+
+    def tops(n, q0, q1):
+        if n == 0:
+            scan(S(0, 0, 32), v("d1"), row("kc", 0), -4 * BIG, A.min, A.max)
+        else:
+            scan(S(n, 32 * q0, 32 * q1), v("d0", 32 * q0, 32 * q1), v("kb", 128 * n + 32 * q0, 128 * n + 32 * q1), -4 * BIG, A.min, A.max)
 
     def below(n, h):
-        if h == 0:
-            ts(v("ebuf", 1, 17), S(n, 0, 16), S(n, 15, 16), A.is_lt, 1.0, A.add)
-        else:
-            ts(v("ebuf", 17, 33), S(n, 16, 32), S(n, 31, 32), A.is_lt)
+        m, c = S(0, 16 * h, 16 * h + 16) if n == 0 else S(n, 32 * h + 1, 32 * h + 32, 2), top(n, h)
+        ts(v("ebuf", 1 + 16 * h, 17 + 16 * h), m, S(n, c, c + 1), A.is_ge if h else A.is_lt, -BIG if h else BIG, A.mult)
 
-    def hot(n, h0, h1):
-        tt(OH(n, h0, h1), v("ebuf", 16 * h0, 16 * h1), v("ebuf", 16 * h0 + 1, 16 * h1 + 1), A.is_gt)
+    def hot(n, h0=0, h1=2):
+        tt(row("oh", n, h0, h1), v("ebuf", 16 * h0, 16 * h1), v("ebuf", 16 * h0 + 1, 16 * h1 + 1), A.subtract)
 
-    def keep(n):
-        tt(v("nd", 64 * n + 1, 64 * n + 64, 2), v("ebuf", 0, 32), v("ebuf", 1, 33), A.is_le)
+    def key_new(n):
+        tt(pair("kb", 128 * (n + 1), 0), row("kc", n), row("oh", n), A.subtract)
+        for h in range(2):
+            c = 128 if h else top(n, 1)
+            ts(pair("kb", 128 * (n + 1), 1, h, h + 1), row("oh", n, h, h + 1), -BIG, A.add, S(n, c, c + 1), A.add)
+
+    def key_join(n):
+        tt(row("kc", n), pair("kb", 128 * n, 0), pair("kb", 128 * n, 1), A.max)
 
     def origin_d(e, n, h):
-        o, c = SW * (n - 1) + 2 + 32 * h, (63, 65)[h]
+        o, c = pair("ib", 64 * n, 1, h, h + 1), (127, 129)[h]
         if e == "a":
-            act(v("ib", o, o + 31, 2), OH(n - 1, h, h + 1), AF.Identity, scale=S(n, c, c + 1))
+            act(o, row("ohn", n - 1, h, h + 1), AF.Identity, scale=S(n, c, c + 1))
         else:
-            ts(v("ib", o, o + 31, 2), OH(n - 1, h, h + 1), S(n, c, c + 1), A.mult)
+            ts(o, row("oh", n - 1, h, h + 1), S(n, c, c + 1), A.min)
 
-    def origin_s(n, h0, h1):
-        scan(v("ib", SW * n + 32 * h0, SW * n + 32 * h1), v("nd", 64 * (n - 1) + 32 * h0, 64 * (n - 1) + 32 * h1),
-             v("ib", SW * (n - 1) + 1 + 32 * h0, SW * (n - 1) + 1 + 32 * h1), 0.0, A.mult, A.add)
+    def origin_join(n):
+        tt(row("ic", n), pair("ib", 64 * n, 0), pair("ib", 64 * n, 1), A.max)
 
-    def origin_p(n, h0, h1):
-        tt(v("kb", 128 * (n + 1) + 65 + 32 * h0, 128 * (n + 1) + 64 + 32 * h1, 2), OH(n, h0, h1),
-           v("ib", SW * n + 1 + 32 * h0, SW * n + 32 * h1, 2), A.mult)
+    def origin_z(n):
+        tt(pair("ib", 64 * n, 0), row("ic", n - 1), row("oh", n - 1), A.subtract)
+
+    def origin_p(n, h0=0, h1=2):
+        for k in range(2):
+            tt(pair("kb", 128 * (n + 1) + 64, k, h0, h1), row("oh", n, h0, h1), pair("ib", 64 * n, k, h0, h1), A.min)
 
     def drawn(e, m):
         for h in range(2):
             c = 32 * (m // 4) + 16 * h + 4 * (m % 4)
-            o, i, b = v("oi", c, c + 4, 1, 0, 32), v("tt", 4 * h, 4 * h + 4, 1, 0, 32), S(m + 1, 47, 48, 1, 0, 32)
+            o, i, b = v("oi", c, c + 4, 1, 0, 32), v("tt", 4 * h, 4 * h + 4, 1, 0, 32), S(m + 1, 95, 96, 1, 0, 32)
             if e == "a":
                 act(o, i, AF.Identity, bias=b)
             else:
@@ -299,44 +317,67 @@ def rank_program(g, core, T, topo):
 
     def quant_x(k, lq, ls):
         quant(half("xq", k), half("xs", k), half("win", k, 4, X0))
-        mm(k, HC, lq, ls, half("xq", k), half("xs", k))
+        mm(k, CUT[k + 1] - CUT[k], lq, ls, half("xq", k), half("xs", k))
 
     W, WB = v("win"), v("win", 0, PAD + 7 * SL)
     for k in range(2):
         quant_x(k, v("urq"), v("urs"))
-    ts(v("sc", SW + 65, None, SW, 96, 128), v("tt", 8, 14, 1, 96, 128), v("pf", 7, 8, 1, 96, 128), A.add)
+    ts(v("sc", SW + 129, None, SW, 96, 128), v("tt", 8, 14, 1, 96, 128), v("pf", 7, 8, 1, 96, 128), A.add)
     tr(v("lt"), v("lr"))
+    units = [lambda b=b: quant(v("eq", 128 * b, 128 * b + 128), v("es", 128 * b, 128 * b + 128),
+                               v("eb" if b % 2 else "ea", 2 - 2 * (b // 2), 514 - 2 * (b // 2))) for b in range(4)]
+    zeros = [lambda k=k: quant(v("lq%d" % k, 0, 128), v("ls%d" % k, 0, 128), v("zero", 0, 512)) for k in range(R)]
+    later = [zeros[0], lambda: memset(v("dd", 0, 256), 0.0), lambda: memset(v("dd", 256), 0.0),
+             lambda: ts(v("pf", 8, 9), v("pf", 2, 3), float(-SL), A.mult, float(X0), A.add),
+             lambda: ts(v("pf", 11, 12), v("pf", 2, 3), 2.0, A.is_ge, float(6 * SL), A.mult),
+             lambda: ts(v("pf", 12, 13), v("pf", 2, 3), float(SL), A.mult, float(SL), A.add)] + units + zeros[1:] + [
+             lambda: quant(v("vq"), v("vs"), v("vt")),
+             lambda: ts(v("pf", 9, 10), v("pf", 7, 8), -6.0, A.mult, float(8 * C), A.add),
+             lambda: ts(v("pf", 10, 11), v("pf", 9, 10), v("pf", 5, 6), A.add)]
+
+    def spare():
+        if later:
+            later.pop(0)()
+
     for t in range(R):
         for k in range(2):
-            tt(half("km", k), v("ps", 512 * k, 512 * k + HC), half("mask", k), A.mult)
+            tt(half("km", k), bank(k, k), half("mask", k), A.mult)
         if t == 0:
             ts(v("bl"), v("tt", 8, 10), v("lt", 0, 1), A.add)
         for k in range(2):
             scan(half("ks", k), half("seg", k), half("km", k), 0.0, A.mult, A.add)
-        tr(v("kb", 1, 64, 2), v("ks", 15, 512, 16))
+        tr(row("kc", 0), v("ks", 15, 512, 16))
         for n in range(V - 1):
-            tops(n, 0, 2 if n == 0 else 4)
-            down(n, "a")
+            tops(n, 0, 2)
+            if n >= 1:
+                tops(n, 2, 4)
+            down(n, "a", 0)
+            if n >= 1:
+                down(n, "a", 1)
             below(n, 0)
             below(n, 1)
             if n >= 1:
+                key_join(n)
                 origin_d("a", n, 0)
                 origin_d("a", n, 1)
-                drawn("a", n - 1)
-            hot(n, 0, 2)
-            keep(n)
-            tt(v("kb", 128 * n + 2, 128 * n + 65, 2), S(n, 0, 65), OH(n), A.mult, off=v("dl", 0, 2))
+                origin_z(n)
+            spare()
+            hot(n)
+            if n < V - 2:
+                act(row("ohn", n), row("oh", n), AF.Copy, scale=1.0 / BIG)
             if n >= 1:
-                origin_s(n, 0, 2)
-            scan(v("kb", 128 * (n + 1), 128 * (n + 1) + 64), v("nd", 64 * n, 64 * n + 64),
-                 v("kb", 128 * n + 1, 128 * n + 65), 0.0, A.mult, A.add)
-            origin_p(n, 0, 2)
+                drawn("a", n - 1)
+            spare()
+            key_new(n)
+            origin_p(n)
+            origin_join(n)
         n = V - 1
-        tops(n, 0, 4)
+        tops(n, 0, 2)
+        tops(n, 2, 4)
         drawn("a", n - 1)
-        origin_d("v", n, 0)
+        origin_z(n)
         below(n, 0)
-        origin_s(n, 0, 1)
+        origin_d("v", n, 0)
         hot(n, 0, 1)
         origin_p(n, 0, 1)
         tops(V, 2, 3)
@@ -362,42 +403,26 @@ def rank_program(g, core, T, topo):
             RemoteDMATransfer(dst_ids=[DstId(rid=rid, pnc=pid)], dma_engine_mask=masks[1], remote_sem=T.sem["arr%d" % t],
                               src=v(bs, 0, HW)[0], dst=v(ls, 128)[0])], local_sem=T.sem["sent"])
         count["sent"] = count.get("sent", 0) + len(es)
-        if t == 0:
-            quant(v(lq, 0, 128), v(ls, 0, 128), v("zero", 0, 512))
-            for b in range(4):
-                o = 2 - 2 * (b // 2)
-                quant(v("eq", 128 * b, 128 * b + 128), v("es", 128 * b, 128 * b + 128), v("eb" if b % 2 else "ea", o, o + 512))
-            memset(v("dd"), 0.0)
-            ts(v("pf", 8, 9), v("pf", 2, 3), float(-SL), A.mult, float(X0), A.add)
-            ts(v("pf", 11, 12), v("pf", 2, 3), 2.0, A.is_ge, float(6 * SL), A.mult)
-        down(n, "v")
+        down(n, "a", 1)
         below(n, 1)
+        down(V, "a", 1)
         origin_d("v", n, 1)
         hot(n, 1, 2)
-        origin_s(n, 1, 2)
-        keep(n)
+        origin_join(n)
         origin_p(n, 1, 2)
-        down(V, "v")
-        tops(V, 3, 4)
         origin_d("v", V, 1)
+        origin_z(V)
+        tops(V, 3, 4)
         origin_d("v", V, 0)
-        origin_s(V, 0, 2)
+        origin_join(V)
         for a in range(4):
-            tr(v("ti", 0, 32, 1, 32 * QG[a], 32 * QG[a] + 32), v("ib", SW * V + 1, SW * V + 64, 2, 32 * a, 32 * a + 32))
-        ts(v("g1", 0, 24), v("ti", 0, 24), v("pf", 8, 9), A.add)
-        ts(v("g2", 0, 24), v("g1", 0, 24), float(X0 + SL), A.is_ge, v("pf", 11, 12), A.mult)
-        tt(v("ti", 0, 24), v("g1", 0, 24), v("g2", 0, 24), A.add)
+            tr(v("ti", 0, 32, 1, 32 * QG[a], 32 * QG[a] + 32), v("ic", 32 * V, 32 * V + 32, 1, 32 * a, 32 * a + 32))
+        ts(v("g2", 0, 24), v("ti", 0, 24), v("pf", 12, 13), A.is_ge, v("pf", 11, 12), A.mult)
+        tt(v("g1", 0, 24), v("ti", 0, 24), v("g2", 0, 24), A.add)
         for k in range(4):
-            ts(v("oz", 24 * k, 24 * k + 24), v("ti", 0, 24), float(k), A.add)
-        if t == 0:
-            for k in range(1, R):
-                quant(v("lq%d" % k, 0, 128), v("ls%d" % k, 0, 128), v("zero", 0, 512))
-        if t == 1:
-            quant(v("vq"), v("vs"), v("vt"))
-            ts(v("pf", 9, 10), v("pf", 7, 8), -6.0, A.mult, float(8 * C), A.add)
-            ts(v("pf", 10, 11), v("pf", 9, 10), v("pf", 5, 6), A.add)
+            ts(v("oz", 24 * k, 24 * k + 24), v("g1", 0, 24), v("pf", 8, 9), A.add, float(k), A.add)
         if t == R - 1:
-            fin = v("ib", SW * V + 1, SW * V + 64, 2)
+            fin = row("ic", V)
             act(v("g1"), fin, AF.Abs, bias=v("pf", 10, 11), scale=6.0)
             ts(v("g2"), fin, 0.25, A.mult)
             tt(v("g2"), v("g2"), v("g1"), A.min)
@@ -422,51 +447,47 @@ def rank_program(g, core, T, topo):
             cp("vav"[a], v("win", HB + 2 * HW * a, HB + 2 * HW * (a + 1), 1, 96, 128), v("win", h3, h3 + 2 * HW, 1, 32 * a, 32 * a + 32))
 
         def fill(e, k, b):
-            cp(e, v("z", 4 * HC * k + b, 4 * HC * (k + 1), 4), W, off=v("oz", 24 * b + 12 * k, 24 * b + 12 * k + 12))
+            cp(e, v("z", 4 * CUT[k] + b, 4 * CUT[k + 1], 4), W, off=v("oz", 24 * b + CUT[k] // 16, 24 * b + CUT[k + 1] // 16))
 
         def layer(k):
             quant(half("zq", k), half("zs", k), half("z", k, 4))
             for b in range(4):
-                mm(4 * k + b, HC, v("wq", 16 + 128 * b, 144 + 128 * b), v("wp", 16 + 128 * b, 144 + 128 * b), half("zq", k), half("zs", k))
+                mm(4 * k + b, CUT[k + 1] - CUT[k], v("wq", 16 + 128 * b, 144 + 128 * b), v("wp", 16 + 128 * b, 144 + 128 * b),
+                   half("zq", k), half("zs", k))
 
         def add(k, b):
-            c0, c1, bank = 4 * HC * k + b, 4 * HC * (k + 1), 512 * (4 * k + b)
-            tt(v("x32", c0, c1, 4), v("ps", bank, bank + HC), v("z32", c0, c1, 4), A.add)
+            c0, c1 = 4 * CUT[k] + b, 4 * CUT[k + 1]
+            tt(v("x32", c0, c1, 4), bank(4 * k + b, k), v("z32", c0, c1, 4), A.add)
 
-        def scale(e, c0, c1):
-            cp(e, v("win", X0 + c0, X0 + c1), v("x32", c0, c1), scale=0.03125)
+        def scale(e, k, b):
+            cp(e, v("win", X0 + 4 * CUT[k] + b, X0 + 4 * CUT[k + 1], 4), v("x32", 4 * CUT[k] + b, 4 * CUT[k + 1], 4), scale=0.03125)
 
-        for e, k, b in (("a", 0, 1), ("v", 0, 0), ("a", 0, 3), ("v", 0, 2), ("a", 1, 1)):
+        for e, k, b in (("a", 0, 1), ("v", 0, 0), ("a", 0, 3), ("v", 0, 2), ("a", 1, 1), ("v", 1, 0)):
             fill(e, k, b)
         layer(0)
-        for e, k, b in (("v", 1, 0), ("a", 1, 3), ("a", 1, 2)):
+        for e, k, b in (("a", 1, 3), ("a", 1, 2)):
             fill(e, k, b)
         cp("v", half("z32", 0, 4), half("z", 0, 4), scale=32.0)
         cp("a", half("z32", 1, 4), half("z", 1, 4), scale=32.0)
-        add(0, 0)
-        add(0, 1)
         layer(1)
-        add(0, 2)
-        add(0, 3)
-        scale("a", 0, 4 * HC)
+        for b in range(4):
+            add(0, b)
+            scale("a", 0, b)
         for b in range(4):
             add(1, b)
-        scale("a", 4 * HC, 6 * HC)
-        scale("v", 6 * HC, 8 * HC)
+        side = (v("urq"), v("urs")) if t < R - 1 else (v("vq"), v("vs"))
+        quant_x(0, *side)
+        cp("v", half("win", 1, 4, X0), half("x32", 1, 4), scale=0.03125)
         if t < R - 1:
             windows(t + 1)
-        for k in range(2):
-            if t < R - 1:
-                quant_x(k, v("urq"), v("urs"))
-            else:
-                quant_x(k, v("vq"), v("vs"))
+        quant_x(1, *side)
 
     dma("s", "so", T.oc[:, :], v("xq")[0].bitcast(dt.uint8), [v("xq")], [])
+    cp("a", half("yt", 0), bank(0, 0))
     for k in range(4):
         i = v("xs", 0, C, 1, 32 * k, 32 * k + 4)
         dma("aass"[k], "so", T.osc[4 * k:4 * k + 4, :], i[0], [i], [])
-    for k in range(2):
-        cp("v", half("yt", k), v("ps", 512 * k, 512 * k + HC))
+    cp("v", half("yt", 1), bank(1, 1))
     dma("a", "so", T.y[:, :], v("yt")[0], [v("yt")], [])
     for sem in SEMAPHORES:
         if count.get(sem, 0) > waited.get(sem, 0):

@@ -11,6 +11,7 @@ NB = 22
 HW = 4 * NB
 WIN = HB + 8 * HW
 BIG = 2.0 ** 96
+STEP = 32768.0
 QG = [0, 2, 1, 3]
 SW = 136
 CUT = [0, 256, C]
@@ -20,9 +21,9 @@ for _d, _l in (
         ("bfloat16", dict(win=WIN, ut=512, vt=512, zero=520, ea=520, eb=520, bt=512, dd=512, z=SL, z32=SL, x32=SL)),
         ("float8_e4m3fn_x4", dict(uq=128, urq=128, vq=128, wq=528, xq=C, zq=C, dq=128, eq=512)),
         ("uint8", dict(us=128, urs=128, vs=128, wp=528, xs=C, zs=C, ds=128, es=512)),
-        ("float32", dict(ci=C, mask=C, seg=C, km=C, ks=512, yt=C, pf=16, d0=128, d1=32, ebuf=40, oh=32 * V, ohn=32 * V, kc=32 * V,
-                         ic=32 * (V + 1), kb=128 * (V + 1), ib=64 * (V + 1), sc=SW * (V + 1), tt=16, oi=64, ot=64,
-                         lr=32, lt=32, ti=32, g1=32, g2=32)),
+        ("float32", dict(ci=C, mask=C, seg=C, km=C, ks=512, yt=C, pf=16, d0=64, ebuf=40, e2=32, i2=32, cc=16, ac=16, na=16, cs=32,
+                         oh=32 * V, ohn=32 * V, kc=32 * V, ic=32 * (V + 1), kb=128 * (V + 1), ib=64 * (V + 1), sc=SW * (V + 1),
+                         tt=16, oi=64, ot=64, lr=32, lt=32, ti=32, g1=32, g2=32)),
         ("int32", dict(pi=8, uli=8)),
         ("uint16", dict(ul=8, bl=2, ob=32, oz=96))):
     for _n, _w in _l.items():
@@ -76,11 +77,14 @@ def rank_program(g, core, T, topo):
             if known[e].get(s, 0) < k:
                 known[e][s] = k
 
-    def deps(e, reads, writes):
+    def deps(e, reads, writes, again=False):
         need = set()
         for _, name, ps, cs in reads:
-            need.update(np.unique(arrs(name)[0][ps, cs]).tolist())
+            if not (again and name == "ps"):
+                need.update(np.unique(arrs(name)[0][ps, cs]).tolist())
         for _, name, ps, cs in writes:
+            if again and name == "ps":
+                continue
             w, r = arrs(name)
             need.update(np.unique(w[ps, cs]).tolist())
             for a in r.values():
@@ -104,9 +108,9 @@ def rank_program(g, core, T, topo):
             for a in r.values():
                 a[ps, cs] = 0
 
-    def op(e, call, reads, writes):
+    def op(e, call, reads, writes, again=False):
         writes = writes + [x for x in reads if x[1] == "ps"]
-        deps(e, reads, writes)
+        deps(e, reads, writes, again)
         sem = csem[e]
         if e == "g":
             wait(e, sem, count.get(sem, 0))
@@ -138,11 +142,11 @@ def rank_program(g, core, T, topo):
         else:
             op("g", lambda: g.iota(o[0], pat, base, cm), [], [o])
 
-    def ts(o, i, s1, op0, s2=None, op1=None, off=None):
+    def ts(o, i, s1, op0, s2=None, op1=None, off=None, again=False):
         if op1 is None:
-            op("v", lambda: g.vector.tensor_scalar(o[0], src(i, off), val(s1), None, op0), aps(i, s1, off), [o])
+            op("v", lambda: g.vector.tensor_scalar(o[0], src(i, off), val(s1), None, op0), aps(i, s1, off), [o], again)
         else:
-            op("v", lambda: g.vector.tensor_scalar(o[0], src(i, off), val(s1), val(s2), op0, op1), aps(i, s1, s2, off), [o])
+            op("v", lambda: g.vector.tensor_scalar(o[0], src(i, off), val(s1), val(s2), op0, op1), aps(i, s1, s2, off), [o], again)
 
     def tt(o, a, b, alu, off=None):
         op("v", lambda: g.vector.tensor_tensor(o[0], src(a, off), b[0], alu), aps(a, b, off), [o])
@@ -153,16 +157,16 @@ def rank_program(g, core, T, topo):
     def tr(o, i):
         op("v", lambda: g.vector.transpose(o[0], i[0]), [i], [o])
 
-    def act(o, i, func, bias=0.0, scale=1.0, off=None):
-        op("a", lambda: g.scalar.activation(o[0], src(i, off), func, bias=val(bias), scale=val(scale)), aps(i, bias, scale, off), [o])
+    def act(o, i, func, bias=0.0, scale=1.0, off=None, again=False):
+        op("a", lambda: g.scalar.activation(o[0], src(i, off), func, bias=val(bias), scale=val(scale)), aps(i, bias, scale, off), [o], again)
 
-    def cp(e, o, i, scale=None, off=None):
+    def cp(e, o, i, scale=None, off=None, again=False):
         if e == "a":
-            act(o, i, AF.Copy, scale=1.0 if scale is None else scale, off=off)
+            act(o, i, AF.Copy, scale=1.0 if scale is None else scale, off=off, again=again)
         elif scale is None:
             op("v", lambda: g.vector.tensor_copy(o[0], src(i, off)), aps(i, off), [o])
         else:
-            ts(o, i, scale, A.mult, off=off)
+            ts(o, i, scale, A.mult, off=off, again=again)
 
     def quant(q, s, i):
         op("v", lambda: g.vector.quantize_mx(q[0], s[0], i[0]), [i], [q, s])
@@ -229,13 +233,13 @@ def rank_program(g, core, T, topo):
     ts(v("pi", 5, 6), p, 31, A.bitwise_and)
     cp("v", v("ul"), v("uli"))
     memset(v("d0"), BIG)
-    memset(v("ebuf", 0, 1), BIG)
-    memset(v("d1"), BIG)
+    memset(v("ebuf", 0, 40, 20), BIG)
+    memset(v("e2"), 0.0)
     cp("v", v("pf", 0, 6), v("pi", 0, 6))
     memset(v("ks", C), 0.0)
     memset(v("ib", 1, 64, 2), 0.0)
-    memset(v("d0", 0, 128, 32), -4 * BIG)
-    memset(v("d1", 0, 32, 16), -4 * BIG)
+    memset(v("d0", 0, 64, 32), -4 * BIG)
+    memset(v("e2", 0, 1), BIG)
     ts(v("pf", 6, 7), v("pf", 3, 4), float(HW), A.mult, float(HB + SL - X0), A.add)
     memset(v("sc", 128, None, SW, 96, 128), -BIG)
     memset(v("oi", p1=32), 0.0)
@@ -253,11 +257,11 @@ def rank_program(g, core, T, topo):
     def S(n, c0, c1, st=1, p0=0, p1=128):
         return v("sc", SW * n + c0, SW * n + c1, st, p0, p1)
 
-    def top(n, h):
-        return (16 if n == 0 else 32) * (h + 1) - 1
+    def top(h):
+        return 16 * h + 15
 
     def down(n, e, k):
-        c = 95 if k else top(n, 0)
+        c = 95 if k else top(0)
         cp(e, S(n, 128 + k, 129 + k, 1, 0, 64), S(n, c, c + 1, 1, 64, 128))
         cp(e, S(n, 128 + k, 129 + k, 1, 64, 96), S(n, c, c + 1, 1, 32, 64))
 
@@ -267,24 +271,24 @@ def rank_program(g, core, T, topo):
     def pair(name, c, k, h0=0, h1=2):
         return v(name, c + 32 * h0 + k, c + 32 * h1, 2)
 
-    def tops(n, q0, q1):
-        if n == 0:
-            scan(S(0, 0, 32), v("d1"), row("kc", 0), -4 * BIG, A.min, A.max)
-        else:
-            scan(S(n, 32 * q0, 32 * q1), v("d0", 32 * q0, 32 * q1), v("kb", 128 * n + 32 * q0, 128 * n + 32 * q1), -4 * BIG, A.min, A.max)
+    def key_top(n, h):
+        a, b = (row("kc", 0, h, h + 1),) * 2 if n == 0 else (pair("kb", 128 * n, 0, h, h + 1), pair("kb", 128 * n, 1, h, h + 1))
+        scan(S(n, 16 * h, 16 * h + 16), a, b, -4 * BIG, A.max, A.max)
 
-    def below(n, h):
-        m, c = S(0, 16 * h, 16 * h + 16) if n == 0 else S(n, 32 * h + 1, 32 * h + 32, 2), top(n, h)
-        ts(v("ebuf", 1 + 16 * h, 17 + 16 * h), m, S(n, c, c + 1), A.is_ge if h else A.is_lt, -BIG if h else BIG, A.mult)
+    def origin_top(n):
+        scan(S(n, 64, 128), v("d0"), v("kb", 128 * n + 64, 128 * n + 128), -4 * BIG, A.min, A.max)
 
-    def hot(n, h0=0, h1=2):
-        tt(row("oh", n, h0, h1), v("ebuf", 16 * h0, 16 * h1), v("ebuf", 16 * h0 + 1, 16 * h1 + 1), A.subtract)
+    def below(n, h, o=None):
+        c = top(h)
+        ts(o or v("ebuf", 1 + 20 * h, 17 + 20 * h), S(n, 16 * h, 16 * h + (15 if o else 16)), S(n, c, c + 1), A.is_lt, BIG, A.mult)
 
-    def key_new(n):
-        tt(pair("kb", 128 * (n + 1), 0), row("kc", n), row("oh", n), A.subtract)
-        for h in range(2):
-            c = 128 if h else top(n, 1)
-            ts(pair("kb", 128 * (n + 1), 1, h, h + 1), row("oh", n, h, h + 1), -BIG, A.add, S(n, c, c + 1), A.add)
+    def hot(n, h):
+        tt(row("oh", n, h, h + 1), v("ebuf", 20 * h, 20 * h + 16), v("ebuf", 20 * h + 1, 20 * h + 17), A.subtract)
+
+    def key_new(n, h):
+        c = 128 if h else top(1)
+        tt(pair("kb", 128 * (n + 1), 0, h, h + 1), row("kc", n, h, h + 1), row("oh", n, h, h + 1), A.subtract)
+        ts(pair("kb", 128 * (n + 1), 1, h, h + 1), row("oh", n, h, h + 1), -BIG, A.add, S(n, c, c + 1), A.add)
 
     def key_join(n):
         tt(row("kc", n), pair("kb", 128 * n, 0), pair("kb", 128 * n, 1), A.max)
@@ -302,18 +306,14 @@ def rank_program(g, core, T, topo):
     def origin_z(n):
         tt(pair("ib", 64 * n, 0), row("ic", n - 1), row("oh", n - 1), A.subtract)
 
-    def origin_p(n, h0=0, h1=2):
+    def origin_p(n):
         for k in range(2):
-            tt(pair("kb", 128 * (n + 1) + 64, k, h0, h1), row("oh", n, h0, h1), pair("ib", 64 * n, k, h0, h1), A.min)
+            tt(pair("kb", 128 * (n + 1) + 64, k), row("oh", n), pair("ib", 64 * n, k), A.min)
 
-    def drawn(e, m):
+    def drawn(m):
         for h in range(2):
             c = 32 * (m // 4) + 16 * h + 4 * (m % 4)
-            o, i, b = v("oi", c, c + 4, 1, 0, 32), v("tt", 4 * h, 4 * h + 4, 1, 0, 32), S(m + 1, 95, 96, 1, 0, 32)
-            if e == "a":
-                act(o, i, AF.Identity, bias=b)
-            else:
-                ts(o, i, b, A.add)
+            act(v("oi", c, c + 4, 1, 0, 32), v("tt", 4 * h, 4 * h + 4, 1, 0, 32), AF.Identity, bias=S(m + 1, 95, 96, 1, 0, 32))
 
     def quant_x(k, lq, ls):
         quant(half("xq", k), half("xs", k), half("win", k, 4, X0))
@@ -327,7 +327,8 @@ def rank_program(g, core, T, topo):
     units = [lambda b=b: quant(v("eq", 128 * b, 128 * b + 128), v("es", 128 * b, 128 * b + 128),
                                v("eb" if b % 2 else "ea", 2 - 2 * (b // 2), 514 - 2 * (b // 2))) for b in range(4)]
     zeros = [lambda k=k: quant(v("lq%d" % k, 0, 128), v("ls%d" % k, 0, 128), v("zero", 0, 512)) for k in range(R)]
-    later = [zeros[0], lambda: memset(v("dd", 0, 256), 0.0), lambda: memset(v("dd", 256), 0.0),
+    later = [lambda: ts(v("cc"), v("ci", 0, 16), STEP, A.mult), zeros[0],
+             lambda: memset(v("dd", 0, 256), 0.0), lambda: memset(v("dd", 256), 0.0),
              lambda: ts(v("pf", 8, 9), v("pf", 2, 3), float(-SL), A.mult, float(X0), A.add),
              lambda: ts(v("pf", 11, 12), v("pf", 2, 3), 2.0, A.is_ge, float(6 * SL), A.mult),
              lambda: ts(v("pf", 12, 13), v("pf", 2, 3), float(SL), A.mult, float(SL), A.add)] + units + zeros[1:] + [
@@ -348,40 +349,58 @@ def rank_program(g, core, T, topo):
             scan(half("ks", k), half("seg", k), half("km", k), 0.0, A.mult, A.add)
         tr(row("kc", 0), v("ks", 15, 512, 16))
         for n in range(V - 1):
-            tops(n, 0, 2)
-            if n >= 1:
-                tops(n, 2, 4)
+            key_top(n, 0)
+            key_top(n, 1)
             down(n, "a", 0)
             if n >= 1:
+                origin_top(n)
                 down(n, "a", 1)
             below(n, 0)
             below(n, 1)
             if n >= 1:
+                origin_join(n - 1)
                 key_join(n)
                 origin_d("a", n, 0)
                 origin_d("a", n, 1)
+            else:
+                spare()
+            hot(n, 0)
+            hot(n, 1)
+            if n >= 1:
                 origin_z(n)
-            spare()
-            hot(n)
+                drawn(n - 1)
             if n < V - 2:
                 act(row("ohn", n), row("oh", n), AF.Copy, scale=1.0 / BIG)
-            if n >= 1:
-                drawn("a", n - 1)
-            spare()
-            key_new(n)
+                spare()
+            else:
+                act(v("na"), row("oh", n, 0, 1), AF.Identity, bias=v("d0", 1, 2), scale=-1.0)
+                scan(v("cs", 0, 16), v("ebuf", 0, 16), v("cc"), 0.0, A.add, A.min)
+            key_new(n, 0)
+            if n < V - 2:
+                key_new(n, 1)
             origin_p(n)
-            origin_join(n)
         n = V - 1
-        tops(n, 0, 2)
-        tops(n, 2, 4)
-        drawn("a", n - 1)
+        key_top(n, 0)
+        origin_join(n - 1)
+        tt(v("ac"), row("oh", n - 1, 0, 1), v("cc"), A.add)
+        origin_top(n)
+        below(n, 0, v("e2", 2, 32, 2))
+        drawn(n - 1)
+        tt(v("i2", 0, 32, 2), row("ic", n - 1, 0, 1), v("ac"), A.add)
+        ts(v("i2", 1, 32, 2), v("na"), S(n, 127, 128), A.add, v("cs", 15, 16), A.add)
+        scan(v("cs", 16, 32), v("e2", 0, 32, 2), v("cc"), 0.0, A.add, A.min)
+        key_new(n - 1, 1)
+        scan(S(V, 0, 32), v("e2"), v("i2"), 0.0, A.add, A.min)
         origin_z(n)
         below(n, 0)
+        key_top(n, 1)
+        for h in range(2):
+            ts(v("oi", 36 + 16 * h, 40 + 16 * h, 1, 0, 32), v("tt", 4 * h, 4 * h + 4, 1, 0, 32), S(V, 31, 32, 1, 0, 32), A.add,
+               v("cs", 31, 32, 1, 0, 32), A.subtract)
+        down(n, "a", 1)
         origin_d("v", n, 0)
-        hot(n, 0, 1)
-        origin_p(n, 0, 1)
-        tops(V, 2, 3)
-        drawn("v", n)
+        hot(n, 0)
+        below(n, 1)
         tr(v("ot", p1=32), v("oi", p1=32))
         cp("v", v("ob"), v("ot"), off=v("bl"))
         cp("a", v("bt", 192, 384), WB, off=v("ob", 16, 28))
@@ -403,48 +422,61 @@ def rank_program(g, core, T, topo):
             RemoteDMATransfer(dst_ids=[DstId(rid=rid, pnc=pid)], dma_engine_mask=masks[1], remote_sem=T.sem["arr%d" % t],
                               src=v(bs, 0, HW)[0], dst=v(ls, 128)[0])], local_sem=T.sem["sent"])
         count["sent"] = count.get("sent", 0) + len(es)
-        down(n, "a", 1)
-        below(n, 1)
-        down(V, "a", 1)
         origin_d("v", n, 1)
-        hot(n, 1, 2)
+        hot(n, 1)
         origin_join(n)
-        origin_p(n, 1, 2)
-        origin_d("v", V, 1)
+        origin_p(n)
         origin_z(V)
-        tops(V, 3, 4)
+        spare()
+        origin_top(V)
+        spare()
+        down(V, "a", 1)
         origin_d("v", V, 0)
+        spare()
+        spare()
+        origin_d("v", V, 1)
+        spare()
         origin_join(V)
+        spare()
         for a in range(4):
             tr(v("ti", 0, 32, 1, 32 * QG[a], 32 * QG[a] + 32), v("ic", 32 * V, 32 * V + 32, 1, 32 * a, 32 * a + 32))
         ts(v("g2", 0, 24), v("ti", 0, 24), v("pf", 12, 13), A.is_ge, v("pf", 11, 12), A.mult)
-        tt(v("g1", 0, 24), v("ti", 0, 24), v("g2", 0, 24), A.add)
-        for k in range(4):
-            ts(v("oz", 24 * k, 24 * k + 24), v("g1", 0, 24), v("pf", 8, 9), A.add, float(k), A.add)
         if t == R - 1:
             fin = row("ic", V)
-            act(v("g1"), fin, AF.Abs, bias=v("pf", 10, 11), scale=6.0)
-            ts(v("g2"), fin, 0.25, A.mult)
-            tt(v("g2"), v("g2"), v("g1"), A.min)
-            for a in range(4):
-                for h in range(2):
-                    i = v("g2", 16 * h, 16 * h + 16, 1, 32 * a, 32 * a + 24)
-                    gg = 2 * QG[a] + h
-                    dma("s", "sg", T.og[gg:gg + 1, :], i[0], [i], [])
+            ts(v("lt"), fin, -6.0, A.mult, v("pf", 10, 11), A.subtract)
+            ts(v("lr"), fin, 6.0, A.mult, v("pf", 10, 11), A.add)
+            ts(v("e2"), fin, 0.25, A.mult)
+        tt(v("g1", 0, 24), v("ti", 0, 24), v("g2", 0, 24), A.add)
+        if t == R - 1:
+            tt(v("i2"), v("lt"), v("lr"), A.max)
         for b in range(4):
             mm(4 + b, 128, v("eq", 128 * b, 128 * b + 128), v("es", 128 * b, 128 * b + 128), v(lq, NB, NB + 128), v(ls, NB, NB + 128))
         for b in range(4):
-            cp("va"[b % 2], v("dd", b, HW, 4), v("ps", 512 * (4 + b) + 128 - NB, 512 * (4 + b) + 128))
+            cp("a", v("dd", b, HW, 4), v("ps", 512 * (4 + b) + 128 - NB, 512 * (4 + b) + 128))
         quant(v("dq"), v("ds"), v("dd"))
+        for k in range(4):
+            ts(v("oz", 24 * k, 24 * k + 24), v("g1", 0, 24), v("pf", 8, 9), A.add, float(k), A.add)
+        if t == R - 1:
+            tt(v("cs"), v("e2"), v("i2"), A.min)
+            for a in range(4):
+                for h in range(2):
+                    i = v("cs", 16 * h, 16 * h + 16, 1, 32 * a, 32 * a + 24)
+                    gg = 2 * QG[a] + h
+                    dma("s", "sg", T.og[gg:gg + 1, :], i[0], [i], [])
         for k in range(8):
             c = 128 * (k % 4) + 16 * (k // 4)
             mm(k, 128, v("wq", c, c + 128), v("wp", c, c + 128), v("dq"), v("ds"))
         h3 = HB + 6 * HW
-        for k in range(8):
-            c = h3 + HW * (k // 4)
-            cp("av"[k % 2], v("win", c + k % 4, c + HW, 4), v("ps", 512 * k, 512 * k + NB), scale=0.03125)
-        for a in range(3):
-            cp("vav"[a], v("win", HB + 2 * HW * a, HB + 2 * HW * (a + 1), 1, 96, 128), v("win", h3, h3 + 2 * HW, 1, 32 * a, 32 * a + 32))
+        for b in range(4):
+            cp("a", v("win", h3 + b, h3 + HW, 4), v("ps", 512 * b, 512 * b + NB), scale=0.03125)
+        for b in range(4):
+            if b == 1:
+                for a in range(3):
+                    cp("v", v("win", HB + 2 * HW * a, HB + 2 * HW * a + HW, 1, 96, 128), v("win", h3, h3 + HW, 1, 32 * a, 32 * a + 32))
+            for a in range(4):
+                c = HB + (2 * a + 1) * HW
+                cp("av"[b % 2], v("win", c + b, c + HW, 4, 96, 128), v("ps", 512 * (4 + b), 512 * (4 + b) + NB, 1, 32 * a, 32 * a + 32),
+                   scale=0.03125, again=a > 0)
 
         def fill(e, k, b):
             cp(e, v("z", 4 * CUT[k] + b, 4 * CUT[k + 1], 4), W, off=v("oz", 24 * b + CUT[k] // 16, 24 * b + CUT[k + 1] // 16))
@@ -472,9 +504,13 @@ def rank_program(g, core, T, topo):
         layer(1)
         for b in range(4):
             add(0, b)
-            scale("a", 0, b)
-        for b in range(4):
-            add(1, b)
+            if b < 3:
+                scale("a", 0, b)
+        add(1, 0)
+        add(1, 1)
+        scale("v", 0, 3)
+        add(1, 2)
+        add(1, 3)
         side = (v("urq"), v("urs")) if t < R - 1 else (v("vq"), v("vs"))
         quant_x(0, *side)
         cp("v", half("win", 1, 4, X0), half("x32", 1, 4), scale=0.03125)

@@ -322,12 +322,12 @@ def rank_program(g, core, T, topo):
     W, WB = v("win"), v("win", 0, PAD + 7 * SL)
     for k in range(2):
         quant_x(k, v("urq"), v("urs"))
-    ts(v("sc", SW + 129, None, SW, 96, 128), v("tt", 8, 14, 1, 96, 128), v("pf", 7, 8, 1, 96, 128), A.add)
-    tr(v("lt"), v("lr"))
     units = [lambda b=b: quant(v("eq", 128 * b, 128 * b + 128), v("es", 128 * b, 128 * b + 128),
                                v("eb" if b % 2 else "ea", 2 - 2 * (b // 2), 514 - 2 * (b // 2))) for b in range(4)]
     zeros = [lambda k=k: quant(v("lq%d" % k, 0, 128), v("ls%d" % k, 0, 128), v("zero", 0, 512)) for k in range(R)]
-    later = [lambda: ts(v("cc"), v("ci", 0, 16), STEP, A.mult), zeros[0],
+    later = [lambda: ts(v("sc", SW + 129, None, SW, 96, 128), v("tt", 8, 14, 1, 96, 128), v("pf", 7, 8, 1, 96, 128), A.add),
+             lambda: tr(v("lt"), v("lr")), lambda: ts(v("cc"), v("ci", 0, 16), STEP, A.mult),
+             lambda: ts(v("bl"), v("tt", 8, 10), v("lt", 0, 1), A.add), zeros[0],
              lambda: memset(v("dd", 0, 256), 0.0), lambda: memset(v("dd", 256), 0.0),
              lambda: ts(v("pf", 8, 9), v("pf", 2, 3), float(-SL), A.mult, float(X0), A.add),
              lambda: ts(v("pf", 11, 12), v("pf", 2, 3), 2.0, A.is_ge, float(6 * SL), A.mult),
@@ -336,15 +336,14 @@ def rank_program(g, core, T, topo):
              lambda: ts(v("pf", 9, 10), v("pf", 7, 8), -6.0, A.mult, float(8 * C), A.add),
              lambda: ts(v("pf", 10, 11), v("pf", 9, 10), v("pf", 5, 6), A.add)]
 
-    def spare():
-        if later:
-            later.pop(0)()
+    def spare(k=1):
+        for _ in range(k):
+            if later:
+                later.pop(0)()
 
     for t in range(R):
         for k in range(2):
             tt(half("km", k), bank(k, k), half("mask", k), A.mult)
-        if t == 0:
-            ts(v("bl"), v("tt", 8, 10), v("lt", 0, 1), A.add)
         for k in range(2):
             scan(half("ks", k), half("seg", k), half("km", k), 0.0, A.mult, A.add)
         tr(row("kc", 0), v("ks", 15, 512, 16))
@@ -355,6 +354,8 @@ def rank_program(g, core, T, topo):
             if n >= 1:
                 origin_top(n)
                 down(n, "a", 1)
+            else:
+                spare(2)
             below(n, 0)
             below(n, 1)
             if n >= 1:
@@ -363,7 +364,7 @@ def rank_program(g, core, T, topo):
                 origin_d("a", n, 0)
                 origin_d("a", n, 1)
             else:
-                spare()
+                spare(2)
             hot(n, 0)
             hot(n, 1)
             if n >= 1:
@@ -402,12 +403,20 @@ def rank_program(g, core, T, topo):
         hot(n, 0)
         below(n, 1)
         tr(v("ot", p1=32), v("oi", p1=32))
+        origin_d("v", n, 1)
+        hot(n, 1)
         cp("v", v("ob"), v("ot"), off=v("bl"))
+        origin_join(n)
+        origin_p(n)
         cp("a", v("bt", 192, 384), WB, off=v("ob", 16, 28))
         cp("v", v("bt", 0, 192), WB, off=v("ob", 0, 12))
+        origin_z(V)
+        origin_top(V)
         cp("v", v("bt", 0, 96, 1, 32, 64), v("bt", 96, 192, 1, 0, 32))
         cp("a", v("bt", 0, 96, 1, 64, 96), v("bt", 192, 288, 1, 0, 32))
         cp("v", v("bt", 0, 96, 1, 96, 128), v("bt", 288, 384, 1, 0, 32))
+        down(V, "a", 1)
+        origin_d("v", V, 0)
         bq, bs, lq, ls = "bq%d" % t, "bs%d" % t, "lq%d" % t, "ls%d" % t
         quant(v(bq), v(bs), v("bt"))
         to = T.cores[(rank + t + 1) % N]
@@ -422,22 +431,11 @@ def rank_program(g, core, T, topo):
             RemoteDMATransfer(dst_ids=[DstId(rid=rid, pnc=pid)], dma_engine_mask=masks[1], remote_sem=T.sem["arr%d" % t],
                               src=v(bs, 0, HW)[0], dst=v(ls, 128)[0])], local_sem=T.sem["sent"])
         count["sent"] = count.get("sent", 0) + len(es)
-        origin_d("v", n, 1)
-        hot(n, 1)
-        origin_join(n)
-        origin_p(n)
-        origin_z(V)
-        spare()
-        origin_top(V)
-        spare()
-        down(V, "a", 1)
-        origin_d("v", V, 0)
-        spare()
-        spare()
+        spare(2)
         origin_d("v", V, 1)
-        spare()
+        spare(2)
         origin_join(V)
-        spare()
+        spare(2)
         for a in range(4):
             tr(v("ti", 0, 32, 1, 32 * QG[a], 32 * QG[a] + 32), v("ic", 32 * V, 32 * V + 32, 1, 32 * a, 32 * a + 32))
         ts(v("g2", 0, 24), v("ti", 0, 24), v("pf", 12, 13), A.is_ge, v("pf", 11, 12), A.mult)
@@ -470,12 +468,12 @@ def rank_program(g, core, T, topo):
         for b in range(4):
             cp("a", v("win", h3 + b, h3 + HW, 4), v("ps", 512 * b, 512 * b + NB), scale=0.03125)
         for b in range(4):
-            if b == 1:
+            if b == 2:
                 for a in range(3):
                     cp("v", v("win", HB + 2 * HW * a, HB + 2 * HW * a + HW, 1, 96, 128), v("win", h3, h3 + HW, 1, 32 * a, 32 * a + 32))
             for a in range(4):
                 c = HB + (2 * a + 1) * HW
-                cp("av"[b % 2], v("win", c + b, c + HW, 4, 96, 128), v("ps", 512 * (4 + b), 512 * (4 + b) + NB, 1, 32 * a, 32 * a + 32),
+                cp("vaav"[b], v("win", c + b, c + HW, 4, 96, 128), v("ps", 512 * (4 + b), 512 * (4 + b) + NB, 1, 32 * a, 32 * a + 32),
                    scale=0.03125, again=a > 0)
 
         def fill(e, k, b):
@@ -511,9 +509,11 @@ def rank_program(g, core, T, topo):
         scale("v", 0, 3)
         add(1, 2)
         add(1, 3)
+        for b in range(3):
+            scale("a", 1, b)
         side = (v("urq"), v("urs")) if t < R - 1 else (v("vq"), v("vs"))
         quant_x(0, *side)
-        cp("v", half("win", 1, 4, X0), half("x32", 1, 4), scale=0.03125)
+        scale("v", 1, 3)
         if t < R - 1:
             windows(t + 1)
         quant_x(1, *side)

@@ -11,9 +11,10 @@ NB = 22
 HW = 4 * NB
 WIN = HB + 8 * HW
 BIG = 2.0 ** 96
-STEP = 32768.0
+LOW = -BIG / 4
+STEP = 32760
 QG = [0, 2, 1, 3]
-SW = 136
+U = 68
 CUT = [0, 256, C]
 
 SCRATCH = {"ps": ("psum", [128, 4096], "float32")}
@@ -21,11 +22,12 @@ for _d, _l in (
         ("bfloat16", dict(win=WIN, ut=512, vt=512, zero=520, ea=520, eb=520, bt=512, dd=512, z=SL, z32=SL, x32=SL)),
         ("float8_e4m3fn_x4", dict(uq=128, urq=128, vq=128, wq=528, xq=C, zq=C, dq=128, eq=512)),
         ("uint8", dict(us=128, urs=128, vs=128, wp=528, xs=C, zs=C, ds=128, es=512)),
-        ("float32", dict(ci=C, mask=C, seg=C, km=C, ks=512, yt=C, pf=16, d0=64, ebuf=40, e2=32, i2=32, cc=16, ac=16, na=16, cs=32,
-                         oh=32 * V, ohn=32 * V, kc=32 * V, ic=32 * (V + 1), kb=128 * (V + 1), ib=64 * (V + 1), sc=SW * (V + 1),
-                         tt=16, oi=64, ot=64, lr=32, lt=32, ti=32, g1=32, g2=32)),
+        ("float32", dict(ci=C, mask=C, seg=C, km=C, ks=512, yt=C, pf=16, kc=32, cc=32, cj=32, fin=32, od=8, pg=4,
+                         pm=U * V, k0=U * V, k1=U * V, ee=U * V, og2=U * (V + 1), rs=U * V, hot=34 * V, nh=34 * V, aa=34 * V,
+                         bb=34 * V, jn=34 * V, sc=8 * V,
+                         tt=16, oi=64, ot=64, lr=32, lt=32, ti=32, g1=32, g2=32, f1=32, f2=32, f3=32)),
         ("int32", dict(pi=8, uli=8)),
-        ("uint16", dict(ul=8, bl=2, ob=32, oz=96))):
+        ("uint16", dict(ul=8, bl=2, ob=32, oz=96, dl=2))):
     for _n, _w in _l.items():
         SCRATCH[_n] = ("sbuf", [128, _w], _d)
 for _t in range(R):
@@ -160,6 +162,9 @@ def rank_program(g, core, T, topo):
     def act(o, i, func, bias=0.0, scale=1.0, off=None, again=False):
         op("a", lambda: g.scalar.activation(o[0], src(i, off), func, bias=val(bias), scale=val(scale)), aps(i, bias, scale, off), [o], again)
 
+    def total(o, i, scale, acc):
+        op("a", lambda: g.scalar.activation(o[0], i[0], AF.Identity, scale=scale, accum_out=acc[0]), [i], [o, acc])
+
     def cp(e, o, i, scale=None, off=None, again=False):
         if e == "a":
             act(o, i, AF.Copy, scale=1.0 if scale is None else scale, off=off, again=again)
@@ -185,7 +190,7 @@ def rank_program(g, core, T, topo):
                 dma(e, sem, o[0], i[0], [i], [o])
         one("s", "we%d" % t, 0, 16, 32, 0)
         for d in range(1, 6):
-            one("a" if t > 0 and d in (2, 4) else "s", "we%d" % t, d + 1, 0, 32, 16 * d)
+            one("s", "we%d" % t, d + 1, 0, 32, 16 * d)
         for d in range(1, 6):
             one("s", "wl%d" % t, d + 7, 32, 128 - 16 * d, 32 + 16 * d)
         one("s", "wl%d" % t, 7, 0, 32, 96)
@@ -216,10 +221,10 @@ def rank_program(g, core, T, topo):
     iota(v("ci"), [[0, 24], [1, 16]], 0, 0)
     memset(v("lr"), 0.0)
     memset(v("zero"), 0.0)
+    memset(v("og2", 1, None, 2), BIG)
     for a in range(4):
-        iota(v("ib", 0, 64, 2, 32 * a, 32 * a + 32), [[SL, 2], [4, 16]], 2 * SL * QG[a], 64)
+        iota(v("og2", 0, U, 2, 32 * a, 32 * a + 32), [[SL, 2], [4 + STEP, 17]], 2 * SL * QG[a], 64)
     iota(v("tt", 8, 14), [[4, 6]], 0, 0)
-    iota(v("tt", 0, 8), [[-SL, 2], [1, 4]], X0, 0)
     for h in range(2):
         iota(v("lr", 16 * h, 16 * h + 12), [[2, 2], [8, 3], [32, 2]], h, 0)
     for name, b in (("ea", 2), ("eb", 3)):
@@ -231,22 +236,24 @@ def rank_program(g, core, T, topo):
     ts(v("pi", 3, 4), p, 7, A.bitwise_and)
     ts(v("pi", 4, 5), p, 3, A.arith_shift_right, 3, A.bitwise_and)
     ts(v("pi", 5, 6), p, 31, A.bitwise_and)
+    ts(v("pi", 6, 7), p, 2, A.arith_shift_right, 3, A.bitwise_and)
     cp("v", v("ul"), v("uli"))
-    memset(v("d0"), BIG)
-    memset(v("ebuf", 0, 40, 20), BIG)
-    memset(v("e2"), 0.0)
-    cp("v", v("pf", 0, 6), v("pi", 0, 6))
+    memset(v("ee"), 0.0)
+    memset(v("k0"), BIG)
+    ts(v("pi", 7, 8), p, 3, A.bitwise_and)
+    cp("v", v("pf", 0, 7), v("pi", 0, 7))
+    cp("v", v("pg", 1, 2), v("pi", 7, 8))
     memset(v("ks", C), 0.0)
-    memset(v("ib", 1, 64, 2), 0.0)
-    memset(v("d0", 0, 64, 32), -4 * BIG)
-    memset(v("e2", 0, 1), BIG)
-    ts(v("pf", 6, 7), v("pf", 3, 4), float(HW), A.mult, float(HB + SL - X0), A.add)
-    memset(v("sc", 128, None, SW, 96, 128), -BIG)
-    memset(v("oi", p1=32), 0.0)
-    memset(v("ot"), 0.0)
+    memset(v("pm", 0, None, U // 2), LOW)
+    memset(v("k1", 33, None, U), LOW)
+    memset(v("k1", U + 32, U + 33), -8 * BIG)
+    memset(v("bb", 16, None, 34), -8 * BIG)
+    memset(v("ee", 0, None, U // 2), BIG)
+    memset(v("k0", 32, None, U), -8 * BIG)
+    ts(v("pf", 13, 14), v("pf", 3, 4), float(HW), A.mult, float(HB + SL - X0), A.add)
+    memset(v("sc", 0, None, 8, 96, 128), LOW)
     memset(v("win", 0, PAD), 0.0)
-    ts(v("pf", 7, 8), v("pf", 4, 5), 32.0, A.mult, v("pf", 6, 7), A.add)
-    memset(v("bt", C), 0.0)
+    ts(v("pf", 7, 8), v("pf", 4, 5), 32.0, A.mult, v("pf", 13, 14), A.add)
     ts(v("mask"), v("ci"), v("pf", 1, 2), A.is_equal)
     act(v("seg"), v("ci"), AF.Sign)
     quant(v("uq"), v("us"), v("ut"))
@@ -254,66 +261,98 @@ def rank_program(g, core, T, topo):
        [v("uq"), v("ul")], [v("urq")])
     op("a", lambda: g.scalar.activation(v("urs")[0], v("us")[0].indirect(v("ul")[0]), AF.Copy), [v("us"), v("ul")], [v("urs")])
 
-    def S(n, c0, c1, st=1, p0=0, p1=128):
-        return v("sc", SW * n + c0, SW * n + c1, st, p0, p1)
+    def pairs(name, n, k, h=None, j=0):
+        c = U * n + k + 2 * j
+        return v(name, c, c + 66, 2) if h is None else v(name, c + 34 * h, c + 34 * h + 32, 2)
 
-    def top(h):
-        return 16 * h + 15
+    def row(name, n, h=None):
+        return v(name, 34 * n, 34 * n + 33) if h is None else v(name, 34 * n + 17 * h, 34 * n + 17 * h + 16)
 
-    def down(n, e, k):
-        c = 95 if k else top(0)
-        cp(e, S(n, 128 + k, 129 + k, 1, 0, 64), S(n, c, c + 1, 1, 64, 128))
-        cp(e, S(n, 128 + k, 129 + k, 1, 64, 96), S(n, c, c + 1, 1, 32, 64))
+    def col(name, c, p0=0, p1=128):
+        return v(name, c, c + 1, 1, p0, p1)
 
-    def row(name, n, h0=0, h1=2):
-        return v(name, 32 * n + 16 * h0, 32 * n + 16 * h1)
+    def top(n, h, p0=0, p1=128):
+        return col("pm", U * n + 34 * h + 32, p0, p1)
 
-    def pair(name, c, k, h0=0, h1=2):
-        return v(name, c + 32 * h0 + k, c + 32 * h1, 2)
+    def came(n, h):
+        return col("sc", 8 * n) if h else top(n, 1)
 
-    def key_top(n, h):
-        a, b = (row("kc", 0, h, h + 1),) * 2 if n == 0 else (pair("kb", 128 * n, 0, h, h + 1), pair("kb", 128 * n, 1, h, h + 1))
-        scan(S(n, 16 * h, 16 * h + 16), a, b, -4 * BIG, A.max, A.max)
+    def place(n, h, p0=0, p1=128):
+        return col("sc", 8 * n + 2 + h, p0, p1)
 
-    def origin_top(n):
-        scan(S(n, 64, 128), v("d0"), v("kb", 128 * n + 64, 128 * n + 128), -4 * BIG, A.min, A.max)
+    def left(n, h, p0=0, p1=128):
+        return col("rs", U * n + 34 * h + 31, p0, p1)
 
-    def below(n, h, o=None):
-        c = top(h)
-        ts(o or v("ebuf", 1 + 20 * h, 17 + 20 * h), S(n, 16 * h, 16 * h + (15 if o else 16)), S(n, c, c + 1), A.is_lt, BIG, A.mult)
+    ACROSS = ((0, 64, 64), (64, 32, 32))
 
-    def hot(n, h):
-        tt(row("oh", n, h, h + 1), v("ebuf", 20 * h, 20 * h + 16), v("ebuf", 20 * h + 1, 20 * h + 17), A.subtract)
+    def key_top(n, h=None):
+        if n == 0:
+            for h in range(2):
+                k = v("kc", 16 * h, 16 * h + 16)
+                scan(pairs("pm", 0, 0, h, 1), k, k, LOW, A.max, A.max)
+        else:
+            c, w = (U * n, 66) if h is None else (U * n + 34 * h, 32)
+            scan(v("pm", c + 1, c + w + 1), v("k0", c, c + w), v("k1", c, c + w), LOW, A.min, A.max)
 
-    def key_new(n, h):
-        c = 128 if h else top(1)
-        tt(pair("kb", 128 * (n + 1), 0, h, h + 1), row("kc", n, h, h + 1), row("oh", n, h, h + 1), A.subtract)
-        ts(pair("kb", 128 * (n + 1), 1, h, h + 1), row("oh", n, h, h + 1), -BIG, A.add, S(n, c, c + 1), A.add)
+    def key_down(n):
+        for to, fr, k in ACROSS:
+            cp("a", col("sc", 8 * n, to, to + k), top(n, 0, fr, fr + k))
+
+    def below(n, h):
+        ts(pairs("ee", n, 0, h, 1), pairs("pm", n, 0, h, 1), top(n, h), A.is_lt, BIG, A.mult)
+
+    def cap(n):
+        tt(pairs("k0", n + 1, 1), pairs("pm", n, 0), pairs("ee", n, 0, None, 1), A.add)
+
+    def rise(n, h):
+        act(pairs("k1", n + 1, 1, h), pairs("ee", n, 0, h, 1), AF.Identity, bias=came(n, h), scale=-1.0)
+
+    def count_to(n, h):
+        total(v("cj", 16 * h, 16 * h + 16), pairs("ee", n, 0, h, 1), STEP / BIG, place(n, h))
+
+    def hot(n):
+        tt(row("hot", n), pairs("ee", n, 0), pairs("ee", n, 0, None, 1), A.subtract)
+
+    def cold(n):
+        act(row("nh", n), row("hot", n), AF.Identity, bias=col("k0", 0), scale=-1.0)
+
+    def key_parts(n):
+        tt(row("aa", n), pairs("k1", n + 1, 0), row("hot", n), A.subtract)
+        for h in range(2):
+            ts(row("bb", n, h), row("hot", n, h), -BIG, A.add, came(n, h), A.add)
 
     def key_join(n):
-        tt(row("kc", n), pair("kb", 128 * n, 0), pair("kb", 128 * n, 1), A.max)
+        tt(pairs("k1", n + 2, 0), row("aa", n), row("bb", n), A.max)
 
-    def origin_d(e, n, h):
-        o, c = pair("ib", 64 * n, 1, h, h + 1), (127, 129)[h]
-        if e == "a":
-            act(o, row("ohn", n - 1, h, h + 1), AF.Identity, scale=S(n, c, c + 1))
-        else:
-            ts(o, row("oh", n - 1, h, h + 1), S(n, c, c + 1), A.min)
+    def origin_top(n, h=None):
+        c, w = (U * n, 66) if h is None else (U * n + 34 * h, 32)
+        scan(v("rs", c, c + w), v("ee", c, c + w), v("og2", c, c + w), 0.0, A.add, A.min)
+
+    def origin_shift(n):
+        act(col("sc", 8 * n + 4), place(n, 1), AF.Identity, bias=place(n, 0), scale=-1.0)
+
+    def origin_down(n, es="aa"):
+        for e, (to, fr, k) in zip(es, ACROSS):
+            o = col("sc", 8 * n + 1, to, to + k)
+            if e == "a":
+                act(o, place(n, 0, fr, fr + k), AF.Identity, bias=left(n, 0, fr, fr + k), scale=-1.0)
+            else:
+                tt(o, left(n, 0, fr, fr + k), place(n, 0, fr, fr + k), A.subtract)
 
     def origin_join(n):
-        tt(row("ic", n), pair("ib", 64 * n, 0), pair("ib", 64 * n, 1), A.max)
+        tt(row("jn", n), pairs("og2", n, 0), pairs("og2", n, 1), A.min)
 
-    def origin_z(n):
-        tt(pair("ib", 64 * n, 0), row("ic", n - 1), row("oh", n - 1), A.subtract)
+    def origin_stay(n):
+        tt(pairs("og2", n + 1, 0), row("jn", n) if n else pairs("og2", 0, 0), row("hot", n), A.max)
 
-    def origin_p(n):
-        for k in range(2):
-            tt(pair("kb", 128 * (n + 1) + 64, k), row("oh", n), pair("ib", 64 * n, k), A.min)
+    def origin_come(n, h):
+        a, b = (col("sc", 8 * n + 1), place(n, 1)) if h else (left(n, 1), col("sc", 8 * n + 4))
+        ts(pairs("og2", n + 1, 1, h), row("nh", n, h), a, A.add, b, A.add)
 
-    def drawn(m):
+    def drawn(n):
         for h in range(2):
-            c = 32 * (m // 4) + 16 * h + 4 * (m % 4)
-            act(v("oi", c, c + 4, 1, 0, 32), v("tt", 4 * h, 4 * h + 4, 1, 0, 32), AF.Identity, bias=S(m + 1, 95, 96, 1, 0, 32))
+            c = 32 * (n // 4) + 16 * h + 4 * (n % 4)
+            ts(v("oi", c, c + 4, 1, 0, 32), v("od", 4, 8, 1, 0, 32), left(n, 0, 0, 32), A.add, place(n, 0, 0, 32), A.subtract)
 
     def quant_x(k, lq, ls):
         quant(half("xq", k), half("xs", k), half("win", k, 4, X0))
@@ -325,98 +364,114 @@ def rank_program(g, core, T, topo):
     units = [lambda b=b: quant(v("eq", 128 * b, 128 * b + 128), v("es", 128 * b, 128 * b + 128),
                                v("eb" if b % 2 else "ea", 2 - 2 * (b // 2), 514 - 2 * (b // 2))) for b in range(4)]
     zeros = [lambda k=k: quant(v("lq%d" % k, 0, 128), v("ls%d" % k, 0, 128), v("zero", 0, 512)) for k in range(R)]
-    later = [lambda: ts(v("sc", SW + 129, None, SW, 96, 128), v("tt", 8, 14, 1, 96, 128), v("pf", 7, 8, 1, 96, 128), A.add),
-             lambda: tr(v("lt"), v("lr")), lambda: ts(v("cc"), v("ci", 0, 16), STEP, A.mult),
-             lambda: ts(v("bl"), v("tt", 8, 10), v("lt", 0, 1), A.add), zeros[0],
-             lambda: memset(v("dd", 0, 256), 0.0), lambda: memset(v("dd", 256), 0.0),
-             lambda: ts(v("pf", 8, 9), v("pf", 2, 3), float(-SL), A.mult, float(X0), A.add),
+    early = [lambda: ts(v("sc", 1, None, 8, 96, 128), v("tt", 8, 14, 1, 96, 128), v("pf", 7, 8, 1, 96, 128), A.add),
+             lambda: tr(v("lt"), v("lr")), lambda: memset(v("od"), 0.0), lambda: memset(v("ot"), 0.0),
+             lambda: memset(v("oi", 32), 0.0),
+             lambda: ts(v("pg", 0, 1), v("pf", 2, 3), 1.0, A.is_equal, float(-SL), A.mult),
+             lambda: ts(v("bl"), v("tt", 8, 10), v("lt", 0, 1), A.add),
+             lambda: ts(v("dl"), v("od", 4, 6), v("pf", 6, 7), A.add),
+             lambda: ts(v("pg", 2, 3), v("pg", 0, 1), v("pg", 1, 2), A.add, float(X0), A.add), lambda: memset(v("bt", C), 0.0),
+             lambda: ts(v("pf", 14, 15), v("pf", 2, 3), float(-SL), A.mult, float(X0), A.add),
              lambda: ts(v("pf", 11, 12), v("pf", 2, 3), 2.0, A.is_ge, float(6 * SL), A.mult),
-             lambda: ts(v("pf", 12, 13), v("pf", 2, 3), float(SL), A.mult, float(SL), A.add)] + units + zeros[1:] + [
-             lambda: quant(v("vq"), v("vs"), v("vt")),
-             lambda: ts(v("pf", 9, 10), v("pf", 7, 8), -6.0, A.mult, float(8 * C), A.add),
-             lambda: ts(v("pf", 10, 11), v("pf", 9, 10), v("pf", 5, 6), A.add)]
+             lambda: ts(v("pf", 15, 16), v("pf", 2, 3), float(SL), A.mult, float(SL), A.add),
+             lambda: ts(v("pf", 8, 9), v("pf", 1, 2), float(-STEP), A.mult, v("pf", 14, 15), A.add),
+             lambda: ts(v("pf", 12, 13), v("pf", 1, 2), float(STEP), A.mult, v("pf", 15, 16), A.add)]
+    later = [zeros[0], lambda: memset(v("dd", 0, 256), 0.0), lambda: memset(v("dd", 256), 0.0)] + units
+    last = zeros[1:] + [
+        lambda: quant(v("vq"), v("vs"), v("vt")), lambda: ts(v("cc"), v("ci", 0, 32), float(STEP), A.mult),
+        lambda: ts(v("pf", 9, 10), v("pf", 7, 8), -6.0, A.mult, float(8 * C), A.add),
+        lambda: ts(v("pf", 10, 11), v("pf", 9, 10), v("pf", 5, 6), A.add)]
 
-    def spare(k=1):
+    def spare(jobs, k=1):
         for _ in range(k):
-            if later:
-                later.pop(0)()
+            if jobs:
+                jobs.pop(0)()
 
     for t in range(R):
         for k in range(2):
             tt(half("km", k), bank(k, k), half("mask", k), A.mult)
         for k in range(2):
             scan(half("ks", k), half("seg", k), half("km", k), 0.0, A.mult, A.add)
-        tr(row("kc", 0), v("ks", 15, 512, 16))
+        spare(early, 3)
+        tr(v("kc"), v("ks", 15, 512, 16))
+        spare(early, 3)
         for n in range(V - 1):
-            key_top(n, 0)
-            key_top(n, 1)
-            down(n, "a", 0)
-            if n >= 1:
-                origin_top(n)
-                down(n, "a", 1)
+            key_top(n)
+            if n == 0:
+                for h in range(2):
+                    cp("a", pairs("k1", 1, 0, h), v("kc", 16 * h, 16 * h + 16))
+                spare(early, 4)
             else:
-                spare(2)
+                cold(n - 1)
+                origin_shift(n - 1)
+                key_parts(n - 1)
+                origin_down(n - 1, "av")
+            key_down(n)
             below(n, 0)
             below(n, 1)
-            if n >= 1:
-                origin_join(n - 1)
-                key_join(n)
-                origin_d("a", n, 0)
-                origin_d("a", n, 1)
-            else:
-                spare(2)
-            hot(n, 0)
-            hot(n, 1)
-            if n >= 1:
-                origin_z(n)
-                drawn(n - 1)
+            rise(n, 0)
             if n < V - 2:
-                act(row("ohn", n), row("oh", n), AF.Copy, scale=1.0 / BIG)
-                spare()
+                rise(n, 1)
+            count_to(n, 0)
+            count_to(n, 1)
+            if n >= 1:
+                act(col("od", n - 1), place(n - 1, 0), AF.Identity, bias=left(n - 1, 0), scale=-1.0)
+                origin_stay(n - 1)
+                origin_come(n - 1, 0)
+                origin_come(n - 1, 1)
+                key_join(n - 1)
             else:
-                act(v("na"), row("oh", n, 0, 1), AF.Identity, bias=v("d0", 1, 2), scale=-1.0)
-                scan(v("cs", 0, 16), v("ebuf", 0, 16), v("cc"), 0.0, A.add, A.min)
-            key_new(n, 0)
+                spare(early, 3)
             if n < V - 2:
-                key_new(n, 1)
-            origin_p(n)
+                cap(n)
+                hot(n)
+            else:
+                rise(n, 1)
+                hot(n)
+                cap(n)
+            if n == 0:
+                spare(early, 2)
+            origin_top(n)
+            if n >= 1:
+                origin_join(n)
         n = V - 1
         key_top(n, 0)
-        origin_join(n - 1)
-        tt(v("ac"), row("oh", n - 1, 0, 1), v("cc"), A.add)
-        origin_top(n)
-        below(n, 0, v("e2", 2, 32, 2))
-        drawn(n - 1)
-        tt(v("i2", 0, 32, 2), row("ic", n - 1, 0, 1), v("ac"), A.add)
-        ts(v("i2", 1, 32, 2), v("na"), S(n, 127, 128), A.add, v("cs", 15, 16), A.add)
-        scan(v("cs", 16, 32), v("e2", 0, 32, 2), v("cc"), 0.0, A.add, A.min)
-        key_new(n - 1, 1)
-        scan(S(V, 0, 32), v("e2"), v("i2"), 0.0, A.add, A.min)
-        origin_z(n)
-        below(n, 0)
+        cold(n - 1)
+        origin_shift(n - 1)
         key_top(n, 1)
-        for h in range(2):
-            ts(v("oi", 36 + 16 * h, 40 + 16 * h, 1, 0, 32), v("tt", 4 * h, 4 * h + 4, 1, 0, 32), S(V, 31, 32, 1, 0, 32), A.add,
-               v("cs", 31, 32, 1, 0, 32), A.subtract)
-        down(n, "a", 1)
-        origin_d("v", n, 0)
-        hot(n, 0)
+        drawn(n - 1)
+        origin_stay(n - 1)
+        origin_down(n - 1)
+        below(n, 0)
+        count_to(n, 0)
+        origin_come(n - 1, 0)
         below(n, 1)
-        tr(v("ot", p1=32), v("oi", p1=32))
-        origin_d("v", n, 1)
-        hot(n, 1)
-        cp("v", v("ob"), v("ot"), off=v("bl"))
+        origin_come(n - 1, 1)
+        cp("a", v("oi", 0, 32), v("od"), off=v("dl"))
+        origin_top(n, 0)
+        count_to(n, 1)
+        hot(n)
+        origin_top(n, 1)
         origin_join(n)
-        origin_p(n)
+        drawn(n)
+        cold(n)
+        origin_shift(n)
+        origin_down(n)
+        origin_stay(n)
+        tr(v("ot", p1=32), v("oi", p1=32))
+        origin_come(n, 0)
+        origin_come(n, 1)
+        ts(v("ob"), v("ot"), v("pg", 2, 3), A.add, off=v("bl"))
+        for h in range(2):
+            tt(v("fin", 16 * h, 16 * h + 16), pairs("og2", V, 0, h), pairs("og2", V, 1, h), A.min)
         cp("a", v("bt", 192, 384), WB, off=v("ob", 16, 28))
         cp("v", v("bt", 0, 192), WB, off=v("ob", 0, 12))
-        origin_z(V)
-        origin_top(V)
+        for a in range(4):
+            tr(v("ti", 0, 32, 1, 32 * QG[a], 32 * QG[a] + 32), v("fin", 0, 32, 1, 32 * a, 32 * a + 32))
         cp("v", v("bt", 0, 96, 1, 32, 64), v("bt", 96, 192, 1, 0, 32))
         cp("a", v("bt", 0, 96, 1, 64, 96), v("bt", 192, 288, 1, 0, 32))
         cp("v", v("bt", 0, 96, 1, 96, 128), v("bt", 288, 384, 1, 0, 32))
-        down(V, "a", 1)
-        origin_d("v", V, 0)
+        ts(v("g2", 0, 24), v("ti", 0, 24), v("pf", 12, 13), A.is_ge, v("pf", 11, 12), A.mult)
         bq, bs, lq, ls = "bq%d" % t, "bs%d" % t, "lq%d" % t, "ls%d" % t
         quant(v(bq), v(bs), v("bt"))
         to = T.cores[(rank + t + 1) % N]
@@ -431,34 +486,28 @@ def rank_program(g, core, T, topo):
             RemoteDMATransfer(dst_ids=[DstId(rid=rid, pnc=pid)], dma_engine_mask=masks[1], remote_sem=T.sem["arr%d" % t],
                               src=v(bs, 0, HW)[0], dst=v(ls, 128)[0])], local_sem=T.sem["sent"])
         count["sent"] = count.get("sent", 0) + len(es)
-        spare(2)
-        origin_d("v", V, 1)
-        spare(2)
-        origin_join(V)
-        spare(2)
-        for a in range(4):
-            tr(v("ti", 0, 32, 1, 32 * QG[a], 32 * QG[a] + 32), v("ic", 32 * V, 32 * V + 32, 1, 32 * a, 32 * a + 32))
-        ts(v("g2", 0, 24), v("ti", 0, 24), v("pf", 12, 13), A.is_ge, v("pf", 11, 12), A.mult)
-        if t == R - 1:
-            fin = row("ic", V)
-            ts(v("lt"), fin, -6.0, A.mult, v("pf", 10, 11), A.subtract)
-            ts(v("lr"), fin, 6.0, A.mult, v("pf", 10, 11), A.add)
-            ts(v("e2"), fin, 0.25, A.mult)
+        spare(later if t == 0 else last, 12)
         tt(v("g1", 0, 24), v("ti", 0, 24), v("g2", 0, 24), A.add)
         if t == R - 1:
-            tt(v("i2"), v("lt"), v("lr"), A.max)
+            tt(v("f3"), v("fin"), v("cc"), A.subtract)
+        for k in range(4):
+            ts(v("oz", 24 * k, 24 * k + 24), v("g1", 0, 24), v("pf", 8, 9), A.add, float(k), A.add)
+        if t == R - 1:
+            ts(v("lt"), v("f3"), -6.0, A.mult, v("pf", 10, 11), A.subtract)
+            ts(v("lr"), v("f3"), 6.0, A.mult, v("pf", 10, 11), A.add)
+            ts(v("f1"), v("f3"), 0.25, A.mult)
+            tt(v("f2"), v("lt"), v("lr"), A.max)
         for b in range(4):
             mm(4 + b, 128, v("eq", 128 * b, 128 * b + 128), v("es", 128 * b, 128 * b + 128), v(lq, NB, NB + 128), v(ls, NB, NB + 128))
         for b in range(4):
             cp("a", v("dd", b, HW, 4), v("ps", 512 * (4 + b) + 128 - NB, 512 * (4 + b) + 128))
-        quant(v("dq"), v("ds"), v("dd"))
-        for k in range(4):
-            ts(v("oz", 24 * k, 24 * k + 24), v("g1", 0, 24), v("pf", 8, 9), A.add, float(k), A.add)
         if t == R - 1:
-            tt(v("cs"), v("e2"), v("i2"), A.min)
+            tt(v("f3"), v("f1"), v("f2"), A.min)
+        quant(v("dq"), v("ds"), v("dd"))
+        if t == R - 1:
             for a in range(4):
                 for h in range(2):
-                    i = v("cs", 16 * h, 16 * h + 16, 1, 32 * a, 32 * a + 24)
+                    i = v("f3", 16 * h, 16 * h + 16, 1, 32 * a, 32 * a + 24)
                     gg = 2 * QG[a] + h
                     dma("s", "sg", T.og[gg:gg + 1, :], i[0], [i], [])
         for k in range(8):

import numpy as np
from concourse.bass import DstId, RemoteDMATransfer
from concourse.mybir import dt, AluOpType, ActivationFunctionType

R, V, C = 3, 6, 384
SL = 4 * C
PAD = 16
X0 = PAD + SL
HB = PAD + 13 * SL
NB = 22
HW = 4 * NB
WIN = HB + 8 * HW
BIG = 2.0 ** 96
LOW = -BIG / 4
STEP = 32760
QG = [0, 2, 1, 3]
U = 68
CUT = [0, 256, C]

SCRATCH = {"ps": ("psum", [128, 4096], "float32")}
for _d, _l in (
        ("bfloat16", dict(win=WIN, ut=512, vt=512, zero=520, ea=520, eb=520, bt=512, dd=512, z=SL, z32=SL, x32=SL)),
        ("float8_e4m3fn_x4", dict(uq=128, urq=128, vq=128, wq=528, xq=C, zq=C, dq=128, eq=512)),
        ("uint8", dict(us=128, urs=128, vs=128, wp=528, xs=C, zs=C, ds=128, es=512)),
        ("float32", dict(ci=C, mask=C, seg=C, km=C, ks=512, yt=C, pf=16, kc=32, cc=32, cj=32, fin=32, od=8, pg=4,
                         pm=U * V, k0=U * V, k1=U * V, ee=U * V, og2=U * (V + 1), rs=U * V, hot=34 * V, nh=34 * V, aa=34 * V,
                         bb=34 * V, jn=34 * V, sc=8 * V,
                         tt=16, oi=64, ot=64, lr=32, lt=32, ti=32, g1=32, g2=32, f1=32, f2=32, f3=32)),
        ("int32", dict(pi=8, uli=8)),
        ("uint16", dict(ul=8, bl=2, ob=32, oz=96, dl=2))):
    for _n, _w in _l.items():
        SCRATCH[_n] = ("sbuf", [128, _w], _d)
for _t in range(R):
    SCRATCH["bq%d" % _t] = ("sbuf", [128, 128], "float8_e4m3fn_x4")
    SCRATCH["bs%d" % _t] = ("sbuf", [128, 128], "uint8")
    SCRATCH["lq%d" % _t] = ("sbuf", [128, 128 + NB], "float8_e4m3fn_x4")
    SCRATCH["ls%d" % _t] = ("sbuf", [128, 128 + HW], "uint8")
SEMAPHORES = ["cv", "ca", "ct", "cg", "sent", "lx0", "lx1", "lu", "lv", "lw", "so", "sg"] + \
    [p + str(t) for p in ("arr", "we", "wl") for t in range(R)]

A = AluOpType
AF = ActivationFunctionType


def rank_program(g, core, T, topo):
    rank = T.rank_of(core)
    if rank is None:
        return
    N = len(T.cores)
    eng = {"v": g.vector, "a": g.scalar, "t": g.tensor, "g": g, "s": g.sync}
    csem = {"v": "cv", "a": "ca", "t": "ct", "g": "cg"}
    count = {}
    known = {e: {} for e in eng}
    waited = {}
    toks = [None]
    lastw, lastr = {}, {}

    def v(name, c0=None, c1=None, st=1, p0=0, p1=128):
        w = SCRATCH[name][1][1]
        c0 = 0 if c0 is None else c0
        c1 = w if c1 is None else c1
        ap = T[name][p0:p1, c0:c1:st] if st != 1 else T[name][p0:p1, c0:c1]
        if name == "ps":
            return (ap, name, slice(0, 8), slice(c0 // 512 * 512, c0 // 512 * 512 + 512))
        return (ap, name, slice(p0 // 16, (p1 + 15) // 16), slice(c0, c1, st))

    def arrs(name):
        if name not in lastw:
            lastw[name] = np.zeros((8, SCRATCH[name][1][1]), np.int32)
            lastr[name] = {}
        return lastw[name], lastr[name]

    def wait(e, sem, n, clock=None):
        if known[e].get(sem, 0) < n:
            eng[e].wait_ge(T.sem[sem], n)
            known[e][sem] = n
            waited[sem] = max(waited.get(sem, 0), n)
        for s, k in (clock or {}).items():
            if known[e].get(s, 0) < k:
                known[e][s] = k

    def deps(e, reads, writes, again=False):
        need = set()
        for _, name, ps, cs in reads:
            if not (again and name == "ps"):
                need.update(np.unique(arrs(name)[0][ps, cs]).tolist())
        for _, name, ps, cs in writes:
            if again and name == "ps":
                continue
            w, r = arrs(name)
            need.update(np.unique(w[ps, cs]).tolist())
            for a in r.values():
                need.update(np.unique(a[ps, cs]).tolist())
        need.discard(0)
        for i in sorted(need, reverse=True):
            sem, n, clock = toks[i]
            wait(e, sem, count[sem] if n is None else n, clock)

    def note(key, tok, reads, writes):
        toks.append(tok)
        i = len(toks) - 1
        for _, name, ps, cs in reads:
            w, r = arrs(name)
            if key not in r:
                r[key] = np.zeros(w.shape, np.int32)
            r[key][ps, cs] = i
        for _, name, ps, cs in writes:
            w, r = arrs(name)
            w[ps, cs] = i
            for a in r.values():
                a[ps, cs] = 0

    def op(e, call, reads, writes, again=False):
        writes = writes + [x for x in reads if x[1] == "ps"]
        deps(e, reads, writes, again)
        sem = csem[e]
        if e == "g":
            wait(e, sem, count.get(sem, 0))
        call().then_inc(T.sem[sem], 1)
        count[sem] = count.get(sem, 0) + 1
        note(e, [sem, count[sem], dict(known[e])], reads, writes)

    def dma(e, sem, out, in_, reads, writes):
        deps(e, reads, writes)
        eng[e].dma_start(out, in_).then_inc(T.sem[sem], 16)
        count[sem] = count.get(sem, 0) + 16
        note(sem, [sem, None, dict(known[e])], reads, writes)

    def aps(*xs):
        return [x for x in xs if isinstance(x, tuple)]

    def val(x):
        return x[0] if isinstance(x, tuple) else x

    def src(x, off):
        return x[0] if off is None else x[0].indirect(off[0])

    def memset(o, c):
        op("v", lambda: g.vector.memset(o[0], c), [], [o])

    def iota(o, pat, base, cm, flt=True):
        if flt:
            op("g", lambda: g.iota(o[0], pat, base, cm, allow_small_or_imprecise_dtypes=True), [], [o])
        else:
            op("g", lambda: g.iota(o[0], pat, base, cm), [], [o])

    def ts(o, i, s1, op0, s2=None, op1=None, off=None, again=False):
        if op1 is None:
            op("v", lambda: g.vector.tensor_scalar(o[0], src(i, off), val(s1), None, op0), aps(i, s1, off), [o], again)
        else:
            op("v", lambda: g.vector.tensor_scalar(o[0], src(i, off), val(s1), val(s2), op0, op1), aps(i, s1, s2, off), [o], again)

    def tt(o, a, b, alu, off=None):
        op("v", lambda: g.vector.tensor_tensor(o[0], src(a, off), b[0], alu), aps(a, b, off), [o])

    def scan(o, d0, d1, init, op0, op1):
        op("v", lambda: g.vector.tensor_tensor_scan(o[0], d0[0], d1[0], init, op0, op1), [d0, d1], [o])

    def tr(o, i):
        op("v", lambda: g.vector.transpose(o[0], i[0]), [i], [o])

    def act(o, i, func, bias=0.0, scale=1.0, off=None, again=False):
        op("a", lambda: g.scalar.activation(o[0], src(i, off), func, bias=val(bias), scale=val(scale)), aps(i, bias, scale, off), [o], again)

    def total(o, i, scale, acc):
        op("a", lambda: g.scalar.activation(o[0], i[0], AF.Identity, scale=scale, accum_out=acc[0]), [i], [o, acc])

    def cp(e, o, i, scale=None, off=None, again=False):
        if e == "a":
            act(o, i, AF.Copy, scale=1.0 if scale is None else scale, off=off, again=again)
        elif scale is None:
            op("v", lambda: g.vector.tensor_copy(o[0], src(i, off)), aps(i, off), [o])
        else:
            ts(o, i, scale, A.mult, off=off, again=again)

    def quant(q, s, i):
        op("v", lambda: g.vector.quantize_mx(q[0], s[0], i[0]), [i], [q, s])

    def mm(bank, n, lq, ls, rq, rs):
        o = v("ps", 512 * bank, 512 * bank + n)
        op("t", lambda: g.tensor.matmul_mx(o[0], lq[0], ls[0], rq[0], rs[0], True, True), [lq, ls, rq, rs], [o])

    def windows(t):
        def one(e, sem, slot, p0, p1, q0):
            o = v("win", PAD + slot * SL, PAD + (slot + 1) * SL, 1, p0, p1)
            if t == 0:
                dma(e, sem, o[0], T.x[q0:q0 + p1 - p0, :], [], [o])
            else:
                i = v("win", X0, X0 + SL, 1, q0, q0 + p1 - p0)
                dma(e, sem, o[0], i[0], [i], [o])
        one("s", "we%d" % t, 0, 16, 32, 0)
        for d in range(1, 6):
            one("s", "we%d" % t, d + 1, 0, 32, 16 * d)
        for d in range(1, 6):
            one("s", "wl%d" % t, d + 7, 32, 128 - 16 * d, 32 + 16 * d)
        one("s", "wl%d" % t, 7, 0, 32, 96)

    def half(name, k, w=1, base=0):
        return v(name, base + w * CUT[k], base + w * CUT[k + 1])

    def bank(b, k):
        return v("ps", 512 * b, 512 * b + CUT[k + 1] - CUT[k])

    for t in range(R):
        count["arr%d" % t] = len(topo.engines(T.cores[(rank - t - 1) % N], core))
        note("arr", ["arr%d" % t, None, {}], [], [v("lq%d" % t, 128), v("ls%d" % t, 128)])

    dma("a", "lu", v("ut")[0], T.u[:, :], [], [v("ut")])
    for k in range(2):
        o = half("win", k, 4, X0)
        dma("s", "lx%d" % k, o[0], T.x[:, 4 * CUT[k]:4 * CUT[k + 1]], [], [o])
    windows(0)
    dma("s", "lw", v("wq", 16)[0].bitcast(dt.uint8), T.wc[:, :], [], [v("wq", 16)])
    dma("s", "lw", v("wp", 16)[0], T.ws[:, :], [], [v("wp", 16)])
    dma("s", "lw", v("wq", 0, 16)[0].bitcast(dt.uint8), T.wc[:, 1984:2048], [], [v("wq", 0, 16)])
    dma("s", "lw", v("wp", 0, 16)[0], T.ws[:, 496:512], [], [v("wp", 0, 16)])
    dma("s", "lv", v("vt")[0], T.v[:, :], [], [v("vt")])

    iota(v("pi", 0, 1), [[0, 1]], 0, 1, False)
    iota(v("uli"), [[32, 2], [64, 2], [16, 2]], 0, 0, False)
    iota(v("ci"), [[0, 24], [1, 16]], 0, 0)
    memset(v("lr"), 0.0)
    memset(v("zero"), 0.0)
    memset(v("og2", 1, None, 2), BIG)
    for a in range(4):
        iota(v("og2", 0, U, 2, 32 * a, 32 * a + 32), [[SL, 2], [4 + STEP, 17]], 2 * SL * QG[a], 64)
    iota(v("tt", 8, 14), [[4, 6]], 0, 0)
    for h in range(2):
        iota(v("lr", 16 * h, 16 * h + 12), [[2, 2], [8, 3], [32, 2]], h, 0)
    for name, b in (("ea", 2), ("eb", 3)):
        op("g", lambda: g.affine_select(v(name, 0, 514)[0], v("zero", 0, 514)[0], [[-1, 514]], A.not_equal, 1.0, b, 4),
           [v("zero", 0, 514)], [v(name, 0, 514)])
    p = v("pi", 0, 1)
    ts(v("pi", 1, 2), p, 15, A.bitwise_and)
    ts(v("pi", 2, 3), p, 4, A.arith_shift_right)
    ts(v("pi", 3, 4), p, 7, A.bitwise_and)
    ts(v("pi", 4, 5), p, 3, A.arith_shift_right, 3, A.bitwise_and)
    ts(v("pi", 5, 6), p, 31, A.bitwise_and)
    ts(v("pi", 6, 7), p, 2, A.arith_shift_right, 3, A.bitwise_and)
    cp("v", v("ul"), v("uli"))
    memset(v("ee"), 0.0)
    memset(v("k0"), BIG)
    ts(v("pi", 7, 8), p, 3, A.bitwise_and)
    cp("v", v("pf", 0, 7), v("pi", 0, 7))
    cp("v", v("pg", 1, 2), v("pi", 7, 8))
    memset(v("ks", C), 0.0)
    memset(v("pm", 0, None, U // 2), LOW)
    memset(v("k1", 33, None, U), LOW)
    memset(v("k1", U + 32, U + 33), -8 * BIG)
    memset(v("bb", 16, None, 34), -8 * BIG)
    memset(v("ee", 0, None, U // 2), BIG)
    memset(v("k0", 32, None, U), -8 * BIG)
    ts(v("pf", 13, 14), v("pf", 3, 4), float(HW), A.mult, float(HB + SL - X0), A.add)
    memset(v("sc", 0, None, 8, 96, 128), LOW)
    memset(v("win", 0, PAD), 0.0)
    ts(v("pf", 7, 8), v("pf", 4, 5), 32.0, A.mult, v("pf", 13, 14), A.add)
    ts(v("mask"), v("ci"), v("pf", 1, 2), A.is_equal)
    act(v("seg"), v("ci"), AF.Sign)
    quant(v("uq"), v("us"), v("ut"))
    op("v", lambda: g.vector.tensor_copy(v("urq")[0].bitcast(dt.uint32), v("uq")[0].bitcast(dt.uint32).indirect(v("ul")[0])),
       [v("uq"), v("ul")], [v("urq")])
    op("a", lambda: g.scalar.activation(v("urs")[0], v("us")[0].indirect(v("ul")[0]), AF.Copy), [v("us"), v("ul")], [v("urs")])

    def pairs(name, n, k, h=None, j=0):
        c = U * n + k + 2 * j
        return v(name, c, c + 66, 2) if h is None else v(name, c + 34 * h, c + 34 * h + 32, 2)

    def row(name, n, h=None):
        return v(name, 34 * n, 34 * n + 33) if h is None else v(name, 34 * n + 17 * h, 34 * n + 17 * h + 16)

    def col(name, c, p0=0, p1=128):
        return v(name, c, c + 1, 1, p0, p1)

    def top(n, h, p0=0, p1=128):
        return col("pm", U * n + 34 * h + 32, p0, p1)

    def came(n, h):
        return col("sc", 8 * n) if h else top(n, 1)

    def place(n, h, p0=0, p1=128):
        return col("sc", 8 * n + 2 + h, p0, p1)

    def left(n, h, p0=0, p1=128):
        return col("rs", U * n + 34 * h + 31, p0, p1)

    ACROSS = ((0, 64, 64), (64, 32, 32))

    def key_top(n, h=None):
        if n == 0:
            for h in range(2):
                k = v("kc", 16 * h, 16 * h + 16)
                scan(pairs("pm", 0, 0, h, 1), k, k, LOW, A.max, A.max)
        else:
            c, w = (U * n, 66) if h is None else (U * n + 34 * h, 32)
            scan(v("pm", c + 1, c + w + 1), v("k0", c, c + w), v("k1", c, c + w), LOW, A.min, A.max)

    def key_down(n):
        for to, fr, k in ACROSS:
            cp("a", col("sc", 8 * n, to, to + k), top(n, 0, fr, fr + k))

    def below(n, h):
        ts(pairs("ee", n, 0, h, 1), pairs("pm", n, 0, h, 1), top(n, h), A.is_lt, BIG, A.mult)

    def cap(n):
        tt(pairs("k0", n + 1, 1), pairs("pm", n, 0), pairs("ee", n, 0, None, 1), A.add)

    def rise(n, h):
        act(pairs("k1", n + 1, 1, h), pairs("ee", n, 0, h, 1), AF.Identity, bias=came(n, h), scale=-1.0)

    def count_to(n, h):
        total(v("cj", 16 * h, 16 * h + 16), pairs("ee", n, 0, h, 1), STEP / BIG, place(n, h))

    def hot(n):
        tt(row("hot", n), pairs("ee", n, 0), pairs("ee", n, 0, None, 1), A.subtract)

    def cold(n):
        act(row("nh", n), row("hot", n), AF.Identity, bias=col("k0", 0), scale=-1.0)

    def key_parts(n):
        tt(row("aa", n), pairs("k1", n + 1, 0), row("hot", n), A.subtract)
        for h in range(2):
            ts(row("bb", n, h), row("hot", n, h), -BIG, A.add, came(n, h), A.add)

    def key_join(n):
        tt(pairs("k1", n + 2, 0), row("aa", n), row("bb", n), A.max)

    def origin_top(n, h=None):
        c, w = (U * n, 66) if h is None else (U * n + 34 * h, 32)
        scan(v("rs", c, c + w), v("ee", c, c + w), v("og2", c, c + w), 0.0, A.add, A.min)

    def origin_shift(n):
        act(col("sc", 8 * n + 4), place(n, 1), AF.Identity, bias=place(n, 0), scale=-1.0)

    def origin_down(n, es="aa"):
        for e, (to, fr, k) in zip(es, ACROSS):
            o = col("sc", 8 * n + 1, to, to + k)
            if e == "a":
                act(o, place(n, 0, fr, fr + k), AF.Identity, bias=left(n, 0, fr, fr + k), scale=-1.0)
            else:
                tt(o, left(n, 0, fr, fr + k), place(n, 0, fr, fr + k), A.subtract)

    def origin_join(n):
        tt(row("jn", n), pairs("og2", n, 0), pairs("og2", n, 1), A.min)

    def origin_stay(n):
        tt(pairs("og2", n + 1, 0), row("jn", n) if n else pairs("og2", 0, 0), row("hot", n), A.max)

    def origin_come(n, h):
        a, b = (col("sc", 8 * n + 1), place(n, 1)) if h else (left(n, 1), col("sc", 8 * n + 4))
        ts(pairs("og2", n + 1, 1, h), row("nh", n, h), a, A.add, b, A.add)

    def drawn(n):
        for h in range(2):
            c = 32 * (n // 4) + 16 * h + 4 * (n % 4)
            ts(v("oi", c, c + 4, 1, 0, 32), v("od", 4, 8, 1, 0, 32), left(n, 0, 0, 32), A.add, place(n, 0, 0, 32), A.subtract)

    def quant_x(k, lq, ls):
        quant(half("xq", k), half("xs", k), half("win", k, 4, X0))
        mm(k, CUT[k + 1] - CUT[k], lq, ls, half("xq", k), half("xs", k))

    W, WB = v("win"), v("win", 0, PAD + 7 * SL)
    for k in range(2):
        quant_x(k, v("urq"), v("urs"))
    units = [lambda b=b: quant(v("eq", 128 * b, 128 * b + 128), v("es", 128 * b, 128 * b + 128),
                               v("eb" if b % 2 else "ea", 2 - 2 * (b // 2), 514 - 2 * (b // 2))) for b in range(4)]
    zeros = [lambda k=k: quant(v("lq%d" % k, 0, 128), v("ls%d" % k, 0, 128), v("zero", 0, 512)) for k in range(R)]
    early = [lambda: ts(v("sc", 1, None, 8, 96, 128), v("tt", 8, 14, 1, 96, 128), v("pf", 7, 8, 1, 96, 128), A.add),
             lambda: tr(v("lt"), v("lr")), lambda: memset(v("od"), 0.0), lambda: memset(v("ot"), 0.0),
             lambda: memset(v("oi", 32), 0.0),
             lambda: ts(v("pg", 0, 1), v("pf", 2, 3), 1.0, A.is_equal, float(-SL), A.mult),
             lambda: ts(v("bl"), v("tt", 8, 10), v("lt", 0, 1), A.add),
             lambda: ts(v("dl"), v("od", 4, 6), v("pf", 6, 7), A.add),
             lambda: ts(v("pg", 2, 3), v("pg", 0, 1), v("pg", 1, 2), A.add, float(X0), A.add), lambda: memset(v("bt", C), 0.0),
             lambda: ts(v("pf", 14, 15), v("pf", 2, 3), float(-SL), A.mult, float(X0), A.add),
             lambda: ts(v("pf", 11, 12), v("pf", 2, 3), 2.0, A.is_ge, float(6 * SL), A.mult),
             lambda: ts(v("pf", 15, 16), v("pf", 2, 3), float(SL), A.mult, float(SL), A.add),
             lambda: ts(v("pf", 8, 9), v("pf", 1, 2), float(-STEP), A.mult, v("pf", 14, 15), A.add),
             lambda: ts(v("pf", 12, 13), v("pf", 1, 2), float(STEP), A.mult, v("pf", 15, 16), A.add)]
    later = [zeros[0], lambda: memset(v("dd", 0, 256), 0.0), lambda: memset(v("dd", 256), 0.0)] + units
    last = zeros[1:] + [
        lambda: quant(v("vq"), v("vs"), v("vt")), lambda: ts(v("cc"), v("ci", 0, 32), float(STEP), A.mult),
        lambda: ts(v("pf", 9, 10), v("pf", 7, 8), -6.0, A.mult, float(8 * C), A.add),
        lambda: ts(v("pf", 10, 11), v("pf", 9, 10), v("pf", 5, 6), A.add)]

    def spare(jobs, k=1):
        for _ in range(k):
            if jobs:
                jobs.pop(0)()

    for t in range(R):
        for k in range(2):
            tt(half("km", k), bank(k, k), half("mask", k), A.mult)
        for k in range(2):
            scan(half("ks", k), half("seg", k), half("km", k), 0.0, A.mult, A.add)
        spare(early, 3)
        tr(v("kc"), v("ks", 15, 512, 16))
        spare(early, 3)
        for n in range(V - 1):
            key_top(n)
            if n == 0:
                for h in range(2):
                    cp("a", pairs("k1", 1, 0, h), v("kc", 16 * h, 16 * h + 16))
                spare(early, 4)
            else:
                cold(n - 1)
                origin_shift(n - 1)
                key_parts(n - 1)
                origin_down(n - 1, "av")
            key_down(n)
            below(n, 0)
            below(n, 1)
            rise(n, 0)
            if n < V - 2:
                rise(n, 1)
            count_to(n, 0)
            count_to(n, 1)
            if n >= 1:
                act(col("od", n - 1), place(n - 1, 0), AF.Identity, bias=left(n - 1, 0), scale=-1.0)
                origin_stay(n - 1)
                origin_come(n - 1, 0)
                origin_come(n - 1, 1)
                key_join(n - 1)
            else:
                spare(early, 3)
            if n < V - 2:
                cap(n)
                hot(n)
            else:
                rise(n, 1)
                hot(n)
                cap(n)
            if n == 0:
                spare(early, 2)
            origin_top(n)
            if n >= 1:
                origin_join(n)
        n = V - 1
        key_top(n, 0)
        cold(n - 1)
        origin_shift(n - 1)
        key_top(n, 1)
        drawn(n - 1)
        origin_stay(n - 1)
        origin_down(n - 1)
        below(n, 0)
        count_to(n, 0)
        origin_come(n - 1, 0)
        below(n, 1)
        origin_come(n - 1, 1)
        cp("a", v("oi", 0, 32), v("od"), off=v("dl"))
        origin_top(n, 0)
        count_to(n, 1)
        hot(n)
        origin_top(n, 1)
        origin_join(n)
        drawn(n)
        cold(n)
        origin_shift(n)
        origin_down(n)
        origin_stay(n)
        tr(v("ot", p1=32), v("oi", p1=32))
        origin_come(n, 0)
        origin_come(n, 1)
        ts(v("ob"), v("ot"), v("pg", 2, 3), A.add, off=v("bl"))
        for h in range(2):
            tt(v("fin", 16 * h, 16 * h + 16), pairs("og2", V, 0, h), pairs("og2", V, 1, h), A.min)
        cp("a", v("bt", 192, 384), WB, off=v("ob", 16, 28))
        cp("v", v("bt", 0, 192), WB, off=v("ob", 0, 12))
        for a in range(4):
            tr(v("ti", 0, 32, 1, 32 * QG[a], 32 * QG[a] + 32), v("fin", 0, 32, 1, 32 * a, 32 * a + 32))
        cp("v", v("bt", 0, 96, 1, 32, 64), v("bt", 96, 192, 1, 0, 32))
        cp("a", v("bt", 0, 96, 1, 64, 96), v("bt", 192, 288, 1, 0, 32))
        cp("v", v("bt", 0, 96, 1, 96, 128), v("bt", 288, 384, 1, 0, 32))
        ts(v("g2", 0, 24), v("ti", 0, 24), v("pf", 12, 13), A.is_ge, v("pf", 11, 12), A.mult)
        bq, bs, lq, ls = "bq%d" % t, "bs%d" % t, "lq%d" % t, "ls%d" % t
        quant(v(bq), v(bs), v("bt"))
        to = T.cores[(rank + t + 1) % N]
        rid, pid, _ = topo.addr(to)
        es = topo.engines(core, to)
        hf = len(es) // 2
        masks = [sum(1 << k for k in es[:hf]), sum(1 << k for k in es[hf:])]
        deps("g", [v(bq), v(bs)], [])
        g.remote_dma_fused([
            RemoteDMATransfer(dst_ids=[DstId(rid=rid, pnc=pid)], dma_engine_mask=masks[0], remote_sem=T.sem["arr%d" % t],
                              src=v(bq, 0, NB)[0].bitcast(dt.uint8), dst=v(lq, 128)[0].bitcast(dt.uint8)),
            RemoteDMATransfer(dst_ids=[DstId(rid=rid, pnc=pid)], dma_engine_mask=masks[1], remote_sem=T.sem["arr%d" % t],
                              src=v(bs, 0, HW)[0], dst=v(ls, 128)[0])], local_sem=T.sem["sent"])
        count["sent"] = count.get("sent", 0) + len(es)
        spare(later if t == 0 else last, 12)
        tt(v("g1", 0, 24), v("ti", 0, 24), v("g2", 0, 24), A.add)
        if t == R - 1:
            tt(v("f3"), v("fin"), v("cc"), A.subtract)
        for k in range(4):
            ts(v("oz", 24 * k, 24 * k + 24), v("g1", 0, 24), v("pf", 8, 9), A.add, float(k), A.add)
        if t == R - 1:
            ts(v("lt"), v("f3"), -6.0, A.mult, v("pf", 10, 11), A.subtract)
            ts(v("lr"), v("f3"), 6.0, A.mult, v("pf", 10, 11), A.add)
            ts(v("f1"), v("f3"), 0.25, A.mult)
            tt(v("f2"), v("lt"), v("lr"), A.max)
        for b in range(4):
            mm(4 + b, 128, v("eq", 128 * b, 128 * b + 128), v("es", 128 * b, 128 * b + 128), v(lq, NB, NB + 128), v(ls, NB, NB + 128))
        for b in range(4):
            cp("a", v("dd", b, HW, 4), v("ps", 512 * (4 + b) + 128 - NB, 512 * (4 + b) + 128))
        if t == R - 1:
            tt(v("f3"), v("f1"), v("f2"), A.min)
        quant(v("dq"), v("ds"), v("dd"))
        if t == R - 1:
            for a in range(4):
                for h in range(2):
                    i = v("f3", 16 * h, 16 * h + 16, 1, 32 * a, 32 * a + 24)
                    gg = 2 * QG[a] + h
                    dma("s", "sg", T.og[gg:gg + 1, :], i[0], [i], [])
        for k in range(8):
            c = 128 * (k % 4) + 16 * (k // 4)
            mm(k, 128, v("wq", c, c + 128), v("wp", c, c + 128), v("dq"), v("ds"))
        h3 = HB + 6 * HW
        for b in range(4):
            cp("a", v("win", h3 + b, h3 + HW, 4), v("ps", 512 * b, 512 * b + NB), scale=0.03125)
        for b in range(4):
            if b == 2:
                for a in range(3):
                    cp("v", v("win", HB + 2 * HW * a, HB + 2 * HW * a + HW, 1, 96, 128), v("win", h3, h3 + HW, 1, 32 * a, 32 * a + 32))
            for a in range(4):
                c = HB + (2 * a + 1) * HW
                cp("vaav"[b], v("win", c + b, c + HW, 4, 96, 128), v("ps", 512 * (4 + b), 512 * (4 + b) + NB, 1, 32 * a, 32 * a + 32),
                   scale=0.03125, again=a > 0)

        def fill(e, k, b):
            cp(e, v("z", 4 * CUT[k] + b, 4 * CUT[k + 1], 4), W, off=v("oz", 24 * b + CUT[k] // 16, 24 * b + CUT[k + 1] // 16))

        def layer(k):
            quant(half("zq", k), half("zs", k), half("z", k, 4))
            for b in range(4):
                mm(4 * k + b, CUT[k + 1] - CUT[k], v("wq", 16 + 128 * b, 144 + 128 * b), v("wp", 16 + 128 * b, 144 + 128 * b),
                   half("zq", k), half("zs", k))

        def add(k, b):
            c0, c1 = 4 * CUT[k] + b, 4 * CUT[k + 1]
            tt(v("x32", c0, c1, 4), bank(4 * k + b, k), v("z32", c0, c1, 4), A.add)

        def scale(e, k, b):
            cp(e, v("win", X0 + 4 * CUT[k] + b, X0 + 4 * CUT[k + 1], 4), v("x32", 4 * CUT[k] + b, 4 * CUT[k + 1], 4), scale=0.03125)

        for e, k, b in (("a", 0, 1), ("v", 0, 0), ("a", 0, 3), ("v", 0, 2), ("a", 1, 1), ("v", 1, 0)):
            fill(e, k, b)
        layer(0)
        for e, k, b in (("a", 1, 3), ("a", 1, 2)):
            fill(e, k, b)
        cp("v", half("z32", 0, 4), half("z", 0, 4), scale=32.0)
        cp("a", half("z32", 1, 4), half("z", 1, 4), scale=32.0)
        layer(1)
        for b in range(4):
            add(0, b)
            if b < 3:
                scale("a", 0, b)
        add(1, 0)
        add(1, 1)
        scale("v", 0, 3)
        add(1, 2)
        add(1, 3)
        for b in range(3):
            scale("a", 1, b)
        side = (v("urq"), v("urs")) if t < R - 1 else (v("vq"), v("vs"))
        quant_x(0, *side)
        scale("v", 1, 3)
        if t < R - 1:
            windows(t + 1)
        quant_x(1, *side)

    dma("s", "so", T.oc[:, :], v("xq")[0].bitcast(dt.uint8), [v("xq")], [])
    cp("a", half("yt", 0), bank(0, 0))
    for k in range(4):
        i = v("xs", 0, C, 1, 32 * k, 32 * k + 4)
        dma("aass"[k], "so", T.osc[4 * k:4 * k + 4, :], i[0], [i], [])
    cp("v", half("yt", 1), bank(1, 1))
    dma("a", "so", T.y[:, :], v("yt")[0], [v("yt")], [])
    for sem in SEMAPHORES:
        if count.get(sem, 0) > waited.get(sem, 0):
            e = "g" if sem == "sent" else "s"
            eng[e].wait_ge(T.sem[sem], count[sem])
